import numpy as np
import ml_dtypes


def mxq(x, axis, fmt="e4m3"):
    dtype, down = {"e4m3": (ml_dtypes.float8_e4m3fn, 7), "e5m2": (ml_dtypes.float8_e5m2, 14)}[fmt]
    v = np.moveaxis(np.asarray(x, np.float32).astype(ml_dtypes.bfloat16).astype(np.float64), axis, -1)
    blocks = v.reshape(v.shape[:-1] + (-1, 32))
    amax = np.abs(blocks).max(-1, keepdims=True)
    byte = np.maximum(np.where(amax > 0, np.frexp(amax)[1] - 1 + 127, 0) - down, 1)
    scale = np.exp2(byte - 127.0)
    codes = (blocks / scale).astype(np.float32).astype(dtype).astype(np.float64)
    return np.moveaxis((codes * scale).reshape(v.shape), -1, axis)


WIDE = False


def mx_kscale(k):
    if not WIDE:
        return np.ones(k)
    levels = np.array([10, -10, 5, -5, 0])
    if k % 512:
        return np.exp2(np.random.permutation(np.resize(levels, k // 32))).repeat(32)
    a = np.empty((k // 512, 16))
    for p in range(k // 512):
        a[p, :8] = np.random.permutation(np.resize(levels, 8))
        for g in range(8):
            far = levels[np.abs(levels - a[p, g]) >= 10]
            a[p, g + 8] = far[np.random.randint(len(far))]
    return np.exp2(a.ravel()).repeat(32)


def f64(x):
    return np.asarray(x).astype(np.float64)


def striped(idx):
    return np.tile(idx.reshape(-1, 16).T, (8, 1)).astype(np.uint16)


def unstriped(offs):
    return offs[:16].T.reshape(-1).astype(np.int64)


def striped8(idx):
    return np.concatenate([x.reshape(-1, 16).T for x in idx]).astype(np.uint16)


def runs(offs, k):
    lists = np.stack([offs[16 * r : 16 * r + 16].T.reshape(-1) for r in range(8)]).astype(np.int64)
    return lists[np.arange(k) % 512 // 64]


def pack_weight(w):
    k, n = w.shape
    w = f64(np.asarray(w, np.float32).astype(ml_dtypes.bfloat16)).reshape(k // 32, 32, n)
    amax = np.abs(w).max(1)
    byte = np.clip(np.where(amax > 0, np.frexp(amax)[1] - 1 + 127 - 7, 1), 1, 254)
    scaled = (w * np.exp2(127.0 - byte)[:, None, :]).reshape(k, n).astype(np.float32)
    words = np.ascontiguousarray(scaled.reshape(k // 512, 128, 4, n).transpose(0, 1, 3, 2)).astype(ml_dtypes.float8_e4m3fn).view(np.uint8)
    return words, np.ascontiguousarray(byte.astype(np.uint8).reshape(k // 512, 16, n))


def unpack_weight(words, scales):
    g, p, n, _ = words.shape
    vals = np.ascontiguousarray(words).view(ml_dtypes.float8_e4m3fn).astype(np.float64) * np.repeat(np.exp2(scales.astype(np.float64) - 127.0), 8, axis=1)[..., None]
    return vals.transpose(0, 1, 3, 2).reshape(g * 512, n)


def sigmoid(v):
    return 1.0 / (1.0 + np.exp(-np.maximum(v, -700.0)))


K, T, S, N, G, H, U = 512, 2048, 512, 512, 2048, 512, 1024


def setup_inputs():
    n = np.random.standard_normal
    s = mx_kscale(K)[:, None]
    u = mx_kscale(H)
    packed_xT = pack_weight(n((K, T)) * s)
    packed_dT = pack_weight(n((K, G)) / s)
    return {
        "x_words": packed_xT[0],
        "x_scales": packed_xT[1],
        "d_words": packed_dT[0],
        "d_scales": packed_dT[1],
        "tab": n((H, U)).astype(np.float32),
        "gn": (np.random.uniform(0.5, 1.5, (H, 1)) * u[:, None]).astype(np.float32),
        "w1": (n((H, N)) / np.sqrt(H) / u[:, None]).astype(np.float32),
        "offs": striped(np.random.permutation(T)[:S]),
        "kidx": striped8(np.random.randint(0, G, (8, H))),
        "rel": striped8(np.random.randint(0, U, (8, S))),
    }


def reference(x_words, x_scales, d_words, d_scales, tab, gn, w1, offs, kidx, rel):
    d_kidx = unpack_weight(d_words, d_scales)[np.arange(K)[:, None], runs(kidx, K)]
    xq = unpack_weight(x_words, x_scales)[:, unstriped(offs)]
    s = 0.0625 * (d_kidx.T @ xq)
    z = f64(gn) * (sigmoid(s + f64(tab)[np.arange(H)[:, None], runs(rel, H)]))
    return mxq(f64(w1), 0, "e4m3").T @ mxq(z, 0, "e4m3")

@@ -1,0 +1,185 @@
+from contextlib import ExitStack
+
+import concourse.mybir as mybir
+
+K, T, S, N, G, H, U = 512, 2048, 512, 512, 2048, 512, 1024
+FLOPS = 2 * K * H * S + 2 * H * N * S
+
+F32 = mybir.dt.float32
+BF16 = mybir.dt.bfloat16
+I32 = mybir.dt.int32
+U32 = mybir.dt.uint32
+U16 = mybir.dt.uint16
+U8 = mybir.dt.uint8
+FP8X4 = mybir.dt.float8_e4m3fn_x4
+ACT = mybir.ActivationFunctionType
+ALU = mybir.AluOpType
+
+P = 128
+PACK = 4
+HALVES = 2
+JW = S // HALVES
+MW = N // 2
+
+
+def tile_picked_scorebias_sigmoid_p_kernel(
+    tc, x_words, x_scales, d_words, d_scales, tab, gn, w1, offs, kidx, rel, out
+):
+    nc = tc.nc
+    with ExitStack() as ctx:
+        lists = ctx.enter_context(tc.tile_pool(name="lists", bufs=1))
+        keep = ctx.enter_context(tc.tile_pool(name="keep", bufs=1))
+        psum = ctx.enter_context(tc.psum_pool(name="psum", bufs=1))
+
+        kidx_t = lists.tile([P, H // 16], U16, name="kidx_t")
+        offs_t = lists.tile([P, S // 16], U16, name="offs_t")
+        rel_t = lists.tile([P, S // 16], U16, name="rel_t")
+
+        ds_win = keep.tile([P, G], U8, name="ds_win", align_bytes=64)
+        xs_win = keep.tile([P, T], U8, name="xs_win", align_bytes=64)
+        dw_win = keep.tile([P, G], I32, name="dw_win", tag="slot_t2", align_bytes=64)
+        xw_win = keep.tile([P, T], I32, name="xw_win", align_bytes=64)
+        planes = keep.tile([P, H + S], U8, name="planes", align_bytes=64)
+        nc.vector.memset(planes[:].bitcast(I32), 0)
+        w_view = w1.rearrange("(p t) m -> p t m", t=PACK)
+        tab_view = tab.rearrange("(p t) u -> t p u", t=PACK)
+
+        nc.sync.dma_start(kidx_t[:], kidx)
+        nc.sync.dma_start(ds_win[:].bitcast(I32), d_scales[0].bitcast(I32).unsqueeze(1).to_broadcast([16, 8, G // 4]))
+        nc.sync.dma_start(offs_t[:], offs)
+        nc.sync.dma_start(xs_win[:].bitcast(I32), x_scales[0].bitcast(I32).unsqueeze(1).to_broadcast([16, 8, T // 4]))
+        nc.sync.dma_start(rel_t[:], rel)
+        nc.sync.dma_start(dw_win[:], d_words[0].rearrange("p n t -> p (n t)").bitcast(I32))
+        nc.sync.dma_start(xw_win[:], x_words[0].rearrange("p n t -> p (n t)").bitcast(I32))
+        gn_t = keep.tile([P, 1, PACK, 1], F32, name="gn_t")
+        nc.gpsimd.dma_start(gn_t[:, 0, :, 0], gn.rearrange("(p t) o -> p (t o)", t=PACK))
+
+        tab_t = []
+
+        def load_tab(t, queue):
+            tab_t.append(keep.tile([P, U], F32, name="tab%d" % t, tag="slot_t%d" % t, align_bytes=64))
+            queue.dma_start(tab_t[t][:], tab_view[t])
+
+        load_tab(0, nc.sync)
+
+        ds_got = keep.tile([P, H], U8, name="ds_got", align_bytes=64)
+        xs_got = keep.tile([P, S], U8, name="xs_got", tag="slot_t1", align_bytes=64)
+        rows = keep.tile([P, H + S], U8, name="rows", tag="slot_w0", align_bytes=64)
+        nc.vector.tensor_copy(ds_got[:], ds_win[:].indirect(kidx_t[:]))
+        nc.vector.tensor_copy(xs_got[:], xs_win[:].indirect(offs_t[:]))
+        nc.vector.tensor_copy(
+            rows[:, 0:H].rearrange("p (t m) -> p m t", t=PACK), ds_got[:].rearrange("p (m t) -> p m t", t=PACK)
+        )
+        nc.vector.tensor_copy(rows[:, H : H + S].bitcast(I32), xs_got[:].bitcast(I32))
+        for a in range(4):
+            nc.scalar.dma_start(planes[a:P:32, :].bitcast(I32), rows[8 * a : P : 32, :].bitcast(I32))
+        load_tab(1, nc.scalar)
+        d_plane = planes[:, 0:H]
+        x_plane = planes[:, H : H + S]
+
+        dw_got = keep.tile([P, H], U32, name="dw_got", tag="slot_t3", align_bytes=64)
+        d_codes = keep.tile([P, H], U32, name="d_codes", tag="stationary", align_bytes=64)
+        nc.vector.tensor_copy(dw_got[:], dw_win[:].bitcast(U32).indirect(kidx_t[:]))
+        load_tab(2, nc.sync)
+        nc.vector.tensor_copy(
+            d_codes[:].rearrange("p (t m) -> p m t", t=PACK), dw_got[:].rearrange("p (m t) -> p m t", t=PACK)
+        )
+        load_tab(3, nc.sync)
+        w_raw = [keep.tile([P, PACK, MW], F32, name="w_raw0", tag="slot_w0", align_bytes=64)]
+        nc.sync.dma_start(w_raw[0][:], w_view[:, :, 0:MW])
+
+        x_codes = [keep.tile([P, JW], U32, name="x_codes%d" % h, tag="slot_x%d" % h, align_bytes=64) for h in range(HALVES)]
+        lw = JW // 16
+        for h in range(HALVES):
+            nc.vector.tensor_copy(x_codes[h][:], xw_win[:].bitcast(U32).indirect(offs_t[:, h * lw : (h + 1) * lw]))
+
+        w_plane = keep.tile([P, N], U8, name="w_plane", align_bytes=64)
+        w_bf = [keep.tile([P, MW * PACK], BF16, name="w_bf%d" % c, align_bytes=64) for c in range(2)]
+
+        def cast_w(c):
+            nc.scalar.copy(
+                w_bf[c][:].rearrange("p (c i t) -> p c t i", i=4, t=PACK),
+                w_raw[c][:].rearrange("p t (c i) -> p c t i", i=4),
+            )
+
+        def quant_w(c):
+            nc.vector.quantize_mx(
+                out=w_codes[:, c * MW : (c + 1) * MW].bitcast(FP8X4), scales=w_plane[:, c * MW : (c + 1) * MW], in_=w_bf[c][:]
+            )
+
+        s_sb = {}
+        for h in range(HALVES):
+            for t in range(PACK):
+                bank = psum.tile([P, JW], F32, name="s_ps", tag="bank%d" % (4 * h + t))
+                nc.tensor.matmul_mx(
+                    out=bank[:],
+                    lhsT=d_codes[:, t * P : (t + 1) * P].bitcast(FP8X4),
+                    lhsT_scale=d_plane[:, t * P : (t + 1) * P],
+                    rhs=x_codes[h][:].bitcast(FP8X4),
+                    rhs_scale=x_plane[:, h * JW : (h + 1) * JW],
+                    start=True,
+                    stop=True,
+                )
+                s_sb[h, t] = (bank, keep.tile([P, JW], F32, name="s_sb%d%d" % (h, t)))
+
+        w_raw.append(keep.tile([P, PACK, MW], F32, name="w_raw1", tag="slot_x0", align_bytes=64))
+        nc.sync.dma_start(w_raw[1][:], w_view[:, :, MW:N])
+        w_codes = keep.tile([P, N], U32, name="w_codes", tag="stationary", align_bytes=64)
+        sig = [keep.tile([P, PACK, JW], F32, name="sig%d" % h) for h in range(HALVES)]
+        order = [(0, 0), (1, 0), (0, 1), (0, 2), (1, 1), (0, 3), (1, 2), (1, 3)]
+
+        def leave(h, t):
+            bank, sb = s_sb[h, t]
+            nc.scalar.activation(sb[:], bank[:], ACT.Copy, scale=0.0625)
+
+        leave(*order[0])
+        leave(*order[1])
+        for n, (h, t) in enumerate(order):
+            if n + 2 < len(order):
+                leave(*order[n + 2])
+            u = keep.tile([P, JW], F32, name="u%d%d" % (h, t))
+            nc.vector.tensor_tensor(u[:], tab_t[t][:].indirect(rel_t[:, h * lw : (h + 1) * lw]), s_sb[h, t][1][:], ALU.add)
+            nc.scalar.activation(sig[h][:, t, :], u[:], ACT.Sigmoid)
+        cast_w(0)
+        cast_w(1)
+
+        z_bf = [keep.tile([P, JW * PACK], BF16, name="z_bf%d" % h, align_bytes=64) for h in range(HALVES)]
+        z_codes = [keep.tile([P, JW], U32, name="z_codes%d" % h, align_bytes=64) for h in range(HALVES)]
+        z_plane = [keep.tile([P, JW], U8, name="z_plane%d" % h, align_bytes=64) for h in range(HALVES)]
+
+        def weigh(h):
+            nc.vector.tensor_tensor(
+                z_bf[h][:].rearrange("p (c i t) -> p c t i", i=4, t=PACK),
+                sig[h][:].rearrange("p t (c i) -> p c t i", i=4),
+                gn_t[:].to_broadcast([P, JW // 4, PACK, 4]),
+                ALU.mult,
+            )
+
+        def quant_z(h):
+            nc.vector.quantize_mx(out=z_codes[h][:].bitcast(FP8X4), scales=z_plane[h][:], in_=z_bf[h][:])
+
+        weigh(0)
+        quant_w(0)
+        quant_z(0)
+        weigh(1)
+        quant_w(1)
+        quant_z(1)
+
+        for h in range(HALVES):
+            for m in range(N // P):
+                bank = psum.tile([P, JW], F32, name="o_ps", tag="bank%d" % (4 * h + m))
+                nc.tensor.matmul_mx(
+                    out=bank[:],
+                    lhsT=w_codes[:, m * P : (m + 1) * P].bitcast(FP8X4),
+                    lhsT_scale=w_plane[:, m * P : (m + 1) * P],
+                    rhs=z_codes[h][:].bitcast(FP8X4),
+                    rhs_scale=z_plane[h][:],
+                    start=True,
+                    stop=True,
+                )
+                res = keep.tile([P, JW], F32, name="res%d%d" % (h, m))
+                if h == 1 and m % 2 == 1:
+                    nc.vector.tensor_copy(res[:], bank[:])
+                else:
+                    nc.scalar.copy(res[:], bank[:])
+                nc.sync.dma_start(out[m * P : (m + 1) * P, h * JW : (h + 1) * JW], res[:])

@@ -17,8 +17,7 @@ ALU = mybir.AluOpType
 
 P = 128
 PACK = 4
-HALVES = 2
-JW = S // HALVES
+JW = S // 2
 MW = N // 2
 
 
@@ -37,62 +36,82 @@ def tile_picked_scorebias_sigmoid_p_kernel(
 
         ds_win = keep.tile([P, G], U8, name="ds_win", align_bytes=64)
         xs_win = keep.tile([P, T], U8, name="xs_win", align_bytes=64)
-        dw_win = keep.tile([P, G], I32, name="dw_win", tag="slot_t2", align_bytes=64)
-        xw_win = keep.tile([P, T], I32, name="xw_win", align_bytes=64)
-        planes = keep.tile([P, H + S], U8, name="planes", align_bytes=64)
-        nc.vector.memset(planes[:].bitcast(I32), 0)
+        dw_win = keep.tile([P, G], I32, name="dw_win", tag="slot_w0", align_bytes=64)
+        xw_win = keep.tile([P, T], I32, name="xw_win", tag="slot_w1", align_bytes=64)
+        nc.vector.memset(ds_win[:].bitcast(I32), 0)
+        nc.gpsimd.memset(xs_win[:].bitcast(I32), 0)
+        warm = keep.tile([P, 2], F32, name="warm")
+        nc.vector.memset(warm[:, 0:1], 0.0)
+        nc.scalar.activation(warm[:, 1:2], warm[:, 0:1], ACT.Sigmoid)
+
         w_view = w1.rearrange("(p t) m -> p t m", t=PACK)
         tab_view = tab.rearrange("(p t) u -> t p u", t=PACK)
 
+        gn_t = keep.tile([P, 1, PACK], F32, name="gn_t")
         nc.sync.dma_start(kidx_t[:], kidx)
-        nc.sync.dma_start(ds_win[:].bitcast(I32), d_scales[0].bitcast(I32).unsqueeze(1).to_broadcast([16, 8, G // 4]))
         nc.sync.dma_start(offs_t[:], offs)
-        nc.sync.dma_start(xs_win[:].bitcast(I32), x_scales[0].bitcast(I32).unsqueeze(1).to_broadcast([16, 8, T // 4]))
         nc.sync.dma_start(rel_t[:], rel)
+        nc.sync.dma_start(gn_t[:, 0, :], gn.rearrange("(p t) o -> p (t o)", t=PACK))
+        nc.sync.dma_start(ds_win[0:P:8, :].bitcast(I32), d_scales[0].bitcast(I32))
+        nc.sync.dma_start(xs_win[0:P:8, :].bitcast(I32), x_scales[0].bitcast(I32))
         nc.sync.dma_start(dw_win[:], d_words[0].rearrange("p n t -> p (n t)").bitcast(I32))
         nc.sync.dma_start(xw_win[:], x_words[0].rearrange("p n t -> p (n t)").bitcast(I32))
-        gn_t = keep.tile([P, 1, PACK, 1], F32, name="gn_t")
-        nc.gpsimd.dma_start(gn_t[:, 0, :, 0], gn.rearrange("(p t) o -> p (t o)", t=PACK))
 
         tab_t = []
 
         def load_tab(t, queue):
-            tab_t.append(keep.tile([P, U], F32, name="tab%d" % t, tag="slot_t%d" % t, align_bytes=64))
+            tab_t.append(keep.tile([P, U], F32, name="tab%d" % t, tag="slot_t%d" % (t % 3), align_bytes=64))
             queue.dma_start(tab_t[t][:], tab_view[t])
 
         load_tab(0, nc.sync)
 
         ds_got = keep.tile([P, H], U8, name="ds_got", align_bytes=64)
         xs_got = keep.tile([P, S], U8, name="xs_got", tag="slot_t1", align_bytes=64)
-        rows = keep.tile([P, H + S], U8, name="rows", tag="slot_w0", align_bytes=64)
+        planes = keep.tile([P, H + S], U8, name="planes", align_bytes=64)
         nc.vector.tensor_copy(ds_got[:], ds_win[:].indirect(kidx_t[:]))
         nc.vector.tensor_copy(xs_got[:], xs_win[:].indirect(offs_t[:]))
         nc.vector.tensor_copy(
-            rows[:, 0:H].rearrange("p (t m) -> p m t", t=PACK), ds_got[:].rearrange("p (m t) -> p m t", t=PACK)
+            planes[:, 0:H].rearrange("p (t m) -> p t m", t=PACK), ds_got[:].rearrange("p (m t) -> p t m", t=PACK)
         )
-        nc.vector.tensor_copy(rows[:, H : H + S].bitcast(I32), xs_got[:].bitcast(I32))
-        for a in range(4):
-            nc.scalar.dma_start(planes[a:P:32, :].bitcast(I32), rows[8 * a : P : 32, :].bitcast(I32))
+        nc.vector.tensor_copy(planes[:, H : H + S].bitcast(I32), xs_got[:].bitcast(I32))
+        for a in range(1, 4):
+            nc.scalar.dma_start(planes[a:P:32, :].bitcast(I32), planes[8 * a : P : 32, :].bitcast(I32))
         load_tab(1, nc.scalar)
         d_plane = planes[:, 0:H]
         x_plane = planes[:, H : H + S]
 
-        dw_got = keep.tile([P, H], U32, name="dw_got", tag="slot_t3", align_bytes=64)
+        dw_got = keep.tile([P, H], U32, name="dw_got", tag="slot_t2", align_bytes=64)
         d_codes = keep.tile([P, H], U32, name="d_codes", tag="stationary", align_bytes=64)
         nc.vector.tensor_copy(dw_got[:], dw_win[:].bitcast(U32).indirect(kidx_t[:]))
-        load_tab(2, nc.sync)
-        nc.vector.tensor_copy(
-            d_codes[:].rearrange("p (t m) -> p m t", t=PACK), dw_got[:].rearrange("p (m t) -> p m t", t=PACK)
-        )
-        load_tab(3, nc.sync)
         w_raw = [keep.tile([P, PACK, MW], F32, name="w_raw0", tag="slot_w0", align_bytes=64)]
         nc.sync.dma_start(w_raw[0][:], w_view[:, :, 0:MW])
+        nc.vector.tensor_copy(
+            d_codes[:].rearrange("p (t c i) -> p c t i", t=PACK, i=4), dw_got[:].rearrange("p (c i t) -> p c t i", t=PACK, i=4)
+        )
+        load_tab(2, nc.sync)
 
-        x_codes = [keep.tile([P, JW], U32, name="x_codes%d" % h, tag="slot_x%d" % h, align_bytes=64) for h in range(HALVES)]
-        lw = JW // 16
-        for h in range(HALVES):
-            nc.vector.tensor_copy(x_codes[h][:], xw_win[:].bitcast(U32).indirect(offs_t[:, h * lw : (h + 1) * lw]))
+        x_codes = [keep.tile([P, JW], U32, name="x_codes%d" % h, align_bytes=64) for h in range(2)]
+        for h in range(2):
+            nc.vector.tensor_copy(
+                x_codes[h][:], xw_win[:].bitcast(U32).indirect(offs_t[:, h * JW // 16 : (h + 1) * JW // 16])
+            )
+        w_raw.append(keep.tile([P, PACK, MW], F32, name="w_raw1", tag="slot_w1", align_bytes=64))
+        nc.sync.dma_start(w_raw[1][:], w_view[:, :, MW:N])
 
+        scores = {}
+        for t, h in [(1, 0), (2, 0), (3, 0), (0, 0), (1, 1), (2, 1), (3, 1), (0, 1)]:
+            scores[t, h] = psum.tile([P, JW], F32, name="s_ps", tag="bank%d" % (2 * t + h))
+            nc.tensor.matmul_mx(
+                out=scores[t, h][:],
+                lhsT=d_codes[:, t * P : (t + 1) * P].bitcast(FP8X4),
+                lhsT_scale=d_plane[:, t * P : (t + 1) * P],
+                rhs=x_codes[h][:].bitcast(FP8X4),
+                rhs_scale=x_plane[:, h * JW : (h + 1) * JW],
+                start=True,
+                stop=True,
+            )
+
+        w_codes = keep.tile([P, N], U32, name="w_codes", tag="stationary", align_bytes=64)
         w_plane = keep.tile([P, N], U8, name="w_plane", align_bytes=64)
         w_bf = [keep.tile([P, MW * PACK], BF16, name="w_bf%d" % c, align_bytes=64) for c in range(2)]
 
@@ -107,79 +126,84 @@ def tile_picked_scorebias_sigmoid_p_kernel(
                 out=w_codes[:, c * MW : (c + 1) * MW].bitcast(FP8X4), scales=w_plane[:, c * MW : (c + 1) * MW], in_=w_bf[c][:]
             )
 
-        s_sb = {}
-        for h in range(HALVES):
-            for t in range(PACK):
-                bank = psum.tile([P, JW], F32, name="s_ps", tag="bank%d" % (4 * h + t))
-                nc.tensor.matmul_mx(
-                    out=bank[:],
-                    lhsT=d_codes[:, t * P : (t + 1) * P].bitcast(FP8X4),
-                    lhsT_scale=d_plane[:, t * P : (t + 1) * P],
-                    rhs=x_codes[h][:].bitcast(FP8X4),
-                    rhs_scale=x_plane[:, h * JW : (h + 1) * JW],
-                    start=True,
-                    stop=True,
-                )
-                s_sb[h, t] = (bank, keep.tile([P, JW], F32, name="s_sb%d%d" % (h, t)))
+        logit = keep.tile([P, PACK, S], F32, name="logit")
+        scaled = [None] + [keep.tile([P, S], F32, name="scaled%d" % t) for t in range(1, PACK)]
 
-        w_raw.append(keep.tile([P, PACK, MW], F32, name="w_raw1", tag="slot_x0", align_bytes=64))
-        nc.sync.dma_start(w_raw[1][:], w_view[:, :, MW:N])
-        w_codes = keep.tile([P, N], U32, name="w_codes", tag="stationary", align_bytes=64)
-        sig = [keep.tile([P, PACK, JW], F32, name="sig%d" % h) for h in range(HALVES)]
-        order = [(0, 0), (1, 0), (0, 1), (0, 2), (1, 1), (0, 3), (1, 2), (1, 3)]
+        def leave(t, h):
+            nc.scalar.activation(scaled[t][:, h * JW : (h + 1) * JW], scores[t, h][:], ACT.Copy, scale=0.0625)
 
-        def leave(h, t):
-            bank, sb = s_sb[h, t]
-            nc.scalar.activation(sb[:], bank[:], ACT.Copy, scale=0.0625)
+        def add_bias(t, a, b):
+            nc.vector.tensor_tensor(logit[:, t, a:b], tab_t[t][:].indirect(rel_t[:, a // 16 : b // 16]), scaled[t][:, a:b], ALU.add)
 
-        leave(*order[0])
-        leave(*order[1])
-        for n, (h, t) in enumerate(order):
-            if n + 2 < len(order):
-                leave(*order[n + 2])
-            u = keep.tile([P, JW], F32, name="u%d%d" % (h, t))
-            nc.vector.tensor_tensor(u[:], tab_t[t][:].indirect(rel_t[:, h * lw : (h + 1) * lw]), s_sb[h, t][1][:], ALU.add)
-            nc.scalar.activation(sig[h][:, t, :], u[:], ACT.Sigmoid)
+        bias0 = keep.tile([P, S], F32, name="bias0")
+        nc.vector.tensor_copy(bias0[:], tab_t[0][:].indirect(rel_t[:]))
+        load_tab(3, nc.sync)
+        for t in range(1, PACK):
+            for h in range(2):
+                leave(t, h)
         cast_w(0)
         cast_w(1)
+        add_bias(1, 0, S)
+        for h in range(2):
+            cols = slice(h * JW, (h + 1) * JW)
+            nc.vector.scalar_tensor_tensor(logit[:, 0, cols], scores[0, h][:], 0.0625, bias0[:, cols], ALU.mult, ALU.add)
+        add_bias(2, 0, S)
+        quant_w(0)
+        add_bias(3, 0, JW)
+        add_bias(3, JW, S)
+        quant_w(1)
 
-        z_bf = [keep.tile([P, JW * PACK], BF16, name="z_bf%d" % h, align_bytes=64) for h in range(HALVES)]
-        z_codes = [keep.tile([P, JW], U32, name="z_codes%d" % h, align_bytes=64) for h in range(HALVES)]
-        z_plane = [keep.tile([P, JW], U8, name="z_plane%d" % h, align_bytes=64) for h in range(HALVES)]
+        QW = S // 4
+        chunks = [(0, 256), (256, 384), (384, 512)]
+        sig = [keep.tile([P, QW, PACK], F32, name="sig%d" % q) for q in range(4)]
+        z_bf = keep.tile([P, S, PACK], BF16, name="z_bf", align_bytes=64)
+        z_codes = [keep.tile([P, b - a], U32, name="z_codes%d" % a, align_bytes=64) for a, b in chunks]
+        z_plane = [keep.tile([P, b - a], U8, name="z_plane%d" % a, align_bytes=64) for a, b in chunks]
 
-        def weigh(h):
-            nc.vector.tensor_tensor(
-                z_bf[h][:].rearrange("p (c i t) -> p c t i", i=4, t=PACK),
-                sig[h][:].rearrange("p t (c i) -> p c t i", i=4),
-                gn_t[:].to_broadcast([P, JW // 4, PACK, 4]),
-                ALU.mult,
+        def weigh(q):
+            nc.scalar.activation(
+                sig[q][:].rearrange("p (c i) t -> p c t i", i=4),
+                logit[:, :, q * QW : (q + 1) * QW].rearrange("p t (c i) -> p c t i", i=4),
+                ACT.Sigmoid,
+            )
+            nc.vector.tensor_tensor(z_bf[:, q * QW : (q + 1) * QW, :], sig[q][:], gn_t[:].to_broadcast([P, QW, PACK]), ALU.mult)
+
+        def quant_z(c):
+            a, b = chunks[c]
+            nc.vector.quantize_mx(
+                out=z_codes[c][:].bitcast(FP8X4), scales=z_plane[c][:], in_=z_bf[:, a:b, :].rearrange("p j t -> p (j t)")
             )
 
-        def quant_z(h):
-            nc.vector.quantize_mx(out=z_codes[h][:].bitcast(FP8X4), scales=z_plane[h][:], in_=z_bf[h][:])
+        out_view = out.rearrange("(m p) j -> p m j", p=P)
 
-        weigh(0)
-        quant_w(0)
-        quant_z(0)
-        weigh(1)
-        quant_w(1)
-        quant_z(1)
-
-        for h in range(HALVES):
-            for m in range(N // P):
-                bank = psum.tile([P, JW], F32, name="o_ps", tag="bank%d" % (4 * h + m))
+        def product(c, pair, engine, queue):
+            a, b = chunks[c]
+            bank = psum.tile([P, 2, b - a], F32, name="o_ps", tag="bank%d" % ((2 * c + pair + 2) % 8))
+            for e in range(2):
+                m = 2 * pair + e
                 nc.tensor.matmul_mx(
-                    out=bank[:],
+                    out=bank[:, e, :],
                     lhsT=w_codes[:, m * P : (m + 1) * P].bitcast(FP8X4),
                     lhsT_scale=w_plane[:, m * P : (m + 1) * P],
-                    rhs=z_codes[h][:].bitcast(FP8X4),
-                    rhs_scale=z_plane[h][:],
+                    rhs=z_codes[c][:].bitcast(FP8X4),
+                    rhs_scale=z_plane[c][:],
                     start=True,
                     stop=True,
                 )
-                res = keep.tile([P, JW], F32, name="res%d%d" % (h, m))
-                if h == 1 and m % 2 == 1:
-                    nc.vector.tensor_copy(res[:], bank[:])
-                else:
-                    nc.scalar.copy(res[:], bank[:])
-                nc.sync.dma_start(out[m * P : (m + 1) * P, h * JW : (h + 1) * JW], res[:])
+            res = keep.tile([P, 2, b - a], F32, name="res%d%d" % (c, pair))
+            engine(res[:], bank[:])
+            queue.dma_start(out_view[:, 2 * pair : 2 * pair + 2, a:b], res[:])
+
+        weigh(0)
+        weigh(1)
+        weigh(2)
+        quant_z(0)
+        weigh(3)
+        quant_z(1)
+        quant_z(2)
+        product(0, 0, nc.scalar.copy, nc.sync)
+        product(0, 1, nc.scalar.copy, nc.sync)
+        product(1, 0, nc.vector.tensor_copy, nc.sync)
+        product(1, 1, nc.vector.tensor_copy, nc.sync)
+        product(2, 0, nc.vector.tensor_copy, nc.sync)
+        product(2, 1, nc.scalar.copy, nc.scalar)

@@ -154,7 +154,7 @@ def tile_picked_scorebias_sigmoid_p_kernel(
         quant_w(1)
 
         QW = S // 4
-        chunks = [(0, 256), (256, 384), (384, 512)]
+        chunks = [(q * QW, (q + 1) * QW) for q in range(4)]
         sig = [keep.tile([P, QW, PACK], F32, name="sig%d" % q) for q in range(4)]
         z_bf = keep.tile([P, S, PACK], BF16, name="z_bf", align_bytes=64)
         z_codes = [keep.tile([P, b - a], U32, name="z_codes%d" % a, align_bytes=64) for a, b in chunks]
@@ -196,14 +196,17 @@ def tile_picked_scorebias_sigmoid_p_kernel(
 
         weigh(0)
         weigh(1)
-        weigh(2)
         quant_z(0)
-        weigh(3)
+        weigh(2)
         quant_z(1)
         quant_z(2)
+        weigh(3)
         product(0, 0, nc.scalar.copy, nc.sync)
-        product(0, 1, nc.scalar.copy, nc.sync)
-        product(1, 0, nc.vector.tensor_copy, nc.sync)
-        product(1, 1, nc.vector.tensor_copy, nc.sync)
-        product(2, 0, nc.vector.tensor_copy, nc.sync)
-        product(2, 1, nc.scalar.copy, nc.scalar)
+        product(0, 1, nc.vector.tensor_copy, nc.sync)
+        quant_z(3)
+        product(1, 0, nc.scalar.copy, nc.sync)
+        product(1, 1, nc.scalar.copy, nc.sync)
+        product(2, 0, nc.scalar.copy, nc.sync)
+        product(2, 1, nc.vector.tensor_copy, nc.sync)
+        product(3, 0, nc.vector.tensor_copy, nc.sync)
+        product(3, 1, nc.scalar.copy, nc.scalar)

@@ -39,7 +39,8 @@ def tile_picked_scorebias_sigmoid_p_kernel(
         dw_win = keep.tile([P, G], I32, name="dw_win", tag="slot_w0", align_bytes=64)
         xw_win = keep.tile([P, T], I32, name="xw_win", tag="slot_w1", align_bytes=64)
         nc.vector.memset(ds_win[:].bitcast(I32), 0)
-        nc.gpsimd.memset(xs_win[:].bitcast(I32), 0)
+        nc.gpsimd.memset(xs_win[:, 0 : T // 2].bitcast(I32), 0)
+        nc.vector.memset(xs_win[:, T // 2 : T].bitcast(I32), 0)
         warm = keep.tile([P, 2], F32, name="warm")
         nc.vector.memset(warm[:, 0:1], 0.0)
         nc.scalar.activation(warm[:, 1:2], warm[:, 0:1], ACT.Sigmoid)
@@ -51,7 +52,6 @@ def tile_picked_scorebias_sigmoid_p_kernel(
         nc.sync.dma_start(kidx_t[:], kidx)
         nc.sync.dma_start(offs_t[:], offs)
         nc.sync.dma_start(rel_t[:], rel)
-        nc.sync.dma_start(gn_t[:, 0, :], gn.rearrange("(p t) o -> p (t o)", t=PACK))
         nc.sync.dma_start(ds_win[0:P:8, :].bitcast(I32), d_scales[0].bitcast(I32))
         nc.sync.dma_start(xs_win[0:P:8, :].bitcast(I32), x_scales[0].bitcast(I32))
         nc.sync.dma_start(dw_win[:], d_words[0].rearrange("p n t -> p (n t)").bitcast(I32))
@@ -64,6 +64,7 @@ def tile_picked_scorebias_sigmoid_p_kernel(
             queue.dma_start(tab_t[t][:], tab_view[t])
 
         load_tab(0, nc.sync)
+        nc.sync.dma_start(gn_t[:, 0, :], gn.rearrange("(p t) o -> p (t o)", t=PACK))
 
         ds_got = keep.tile([P, H], U8, name="ds_got", align_bytes=64)
         xs_got = keep.tile([P, S], U8, name="xs_got", tag="slot_t1", align_bytes=64)

@@ -19,6 +19,7 @@ P = 128
 PACK = 4
 JW = S // 2
 MW = N // 2
+TAB_AT = [16 * U, 0, 8 * U, 20 * U]
 
 
 def tile_picked_scorebias_sigmoid_p_kernel(
@@ -28,6 +29,7 @@ def tile_picked_scorebias_sigmoid_p_kernel(
     with ExitStack() as ctx:
         lists = ctx.enter_context(tc.tile_pool(name="lists", bufs=1))
         keep = ctx.enter_context(tc.tile_pool(name="keep", bufs=1))
+        placed = ctx.enter_context(tc.tile_pool(name="placed", bufs=1))
         psum = ctx.enter_context(tc.psum_pool(name="psum", bufs=1))
 
         kidx_t = lists.tile([P, H // 16], U16, name="kidx_t")
@@ -36,11 +38,11 @@ def tile_picked_scorebias_sigmoid_p_kernel(
 
         ds_win = keep.tile([P, G], U8, name="ds_win", align_bytes=64)
         xs_win = keep.tile([P, T], U8, name="xs_win", align_bytes=64)
-        dw_win = keep.tile([P, G], I32, name="dw_win", tag="slot_w0", align_bytes=64)
+        dw_win = placed.tile([P, G], I32, name="dw_win", offset=8 * U, align_bytes=64)
         xw_win = keep.tile([P, T], I32, name="xw_win", tag="slot_w1", align_bytes=64)
-        nc.vector.memset(ds_win[:].bitcast(I32), 0)
-        nc.gpsimd.memset(xs_win[:, 0 : T // 2].bitcast(I32), 0)
-        nc.vector.memset(xs_win[:, T // 2 : T].bitcast(I32), 0)
+        for win in (ds_win, xs_win):
+            nc.gpsimd.memset(win[:, 0 : T // 2].bitcast(I32), 0)
+            nc.vector.memset(win[:, T // 2 : T].bitcast(I32), 0)
         warm = keep.tile([P, 2], F32, name="warm")
         nc.vector.memset(warm[:, 0:1], 0.0)
         nc.scalar.activation(warm[:, 1:2], warm[:, 0:1], ACT.Sigmoid)
@@ -48,26 +50,26 @@ def tile_picked_scorebias_sigmoid_p_kernel(
         w_view = w1.rearrange("(p t) m -> p t m", t=PACK)
         tab_view = tab.rearrange("(p t) u -> t p u", t=PACK)
 
-        gn_t = keep.tile([P, 1, PACK], F32, name="gn_t")
         nc.sync.dma_start(kidx_t[:], kidx)
         nc.sync.dma_start(offs_t[:], offs)
-        nc.sync.dma_start(rel_t[:], rel)
+        d_src = d_words[0].rearrange("p n t -> p (n t)").bitcast(I32)
+        nc.sync.dma_start(dw_win[:, 0 : G // 4], d_src[:, 0 : G // 4])
         nc.sync.dma_start(ds_win[0:P:8, :].bitcast(I32), d_scales[0].bitcast(I32))
         nc.sync.dma_start(xs_win[0:P:8, :].bitcast(I32), x_scales[0].bitcast(I32))
-        nc.sync.dma_start(dw_win[:], d_words[0].rearrange("p n t -> p (n t)").bitcast(I32))
+        nc.sync.dma_start(dw_win[:, G // 4 : G], d_src[:, G // 4 : G])
         nc.sync.dma_start(xw_win[:], x_words[0].rearrange("p n t -> p (n t)").bitcast(I32))
 
         tab_t = []
 
         def load_tab(t, queue):
-            tab_t.append(keep.tile([P, U], F32, name="tab%d" % t, tag="slot_t%d" % (t % 3), align_bytes=64))
+            tab_t.append(placed.tile([P, U], F32, name="tab%d" % t, offset=TAB_AT[t], align_bytes=64))
             queue.dma_start(tab_t[t][:], tab_view[t])
 
         load_tab(0, nc.sync)
-        nc.sync.dma_start(gn_t[:, 0, :], gn.rearrange("(p t) o -> p (t o)", t=PACK))
+        nc.sync.dma_start(rel_t[:], rel)
 
         ds_got = keep.tile([P, H], U8, name="ds_got", align_bytes=64)
-        xs_got = keep.tile([P, S], U8, name="xs_got", tag="slot_t1", align_bytes=64)
+        xs_got = placed.tile([P, S], U8, name="xs_got", offset=4 * U - S // 2, align_bytes=64)
         planes = keep.tile([P, H + S], U8, name="planes", align_bytes=64)
         nc.vector.tensor_copy(ds_got[:], ds_win[:].indirect(kidx_t[:]))
         nc.vector.tensor_copy(xs_got[:], xs_win[:].indirect(offs_t[:]))
@@ -78,32 +80,35 @@ def tile_picked_scorebias_sigmoid_p_kernel(
         for a in range(1, 4):
             nc.scalar.dma_start(planes[a:P:32, :].bitcast(I32), planes[8 * a : P : 32, :].bitcast(I32))
         load_tab(1, nc.scalar)
+        w_raw = [placed.tile([P, PACK, MW], F32, name="w_raw0", offset=4 * U, align_bytes=64)]
+        nc.scalar.dma_start(w_raw[0][:], w_view[:, :, 0:MW])
         d_plane = planes[:, 0:H]
         x_plane = planes[:, H : H + S]
 
-        dw_got = keep.tile([P, H], U32, name="dw_got", tag="slot_t2", align_bytes=64)
+        dw_got = placed.tile([P, H], U32, name="dw_got", offset=23 * U, align_bytes=64)
         d_codes = keep.tile([P, H], U32, name="d_codes", tag="stationary", align_bytes=64)
         nc.vector.tensor_copy(dw_got[:], dw_win[:].bitcast(U32).indirect(kidx_t[:]))
-        w_raw = [keep.tile([P, PACK, MW], F32, name="w_raw0", tag="slot_w0", align_bytes=64)]
-        nc.sync.dma_start(w_raw[0][:], w_view[:, :, 0:MW])
+        load_tab(2, nc.sync)
+        w_raw.append(placed.tile([P, PACK, MW], F32, name="w_raw1", offset=12 * U, align_bytes=64))
+        nc.sync.dma_start(w_raw[1][:], w_view[:, :, MW:N])
         nc.vector.tensor_copy(
             d_codes[:].rearrange("p (t c i) -> p c t i", t=PACK, i=4), dw_got[:].rearrange("p (c i t) -> p c t i", t=PACK, i=4)
         )
-        load_tab(2, nc.sync)
+        load_tab(3, nc.sync)
+        gn_t = placed.tile([P, 1, PACK], F32, name="gn_t", offset=24 * U, align_bytes=64)
+        nc.sync.dma_start(gn_t[:, 0, :], gn.rearrange("(p t) o -> p (t o)", t=PACK))
 
         x_codes = [keep.tile([P, JW], U32, name="x_codes%d" % h, align_bytes=64) for h in range(2)]
         for h in range(2):
             nc.vector.tensor_copy(
                 x_codes[h][:], xw_win[:].bitcast(U32).indirect(offs_t[:, h * JW // 16 : (h + 1) * JW // 16])
             )
-        w_raw.append(keep.tile([P, PACK, MW], F32, name="w_raw1", tag="slot_w1", align_bytes=64))
-        nc.sync.dma_start(w_raw[1][:], w_view[:, :, MW:N])
 
-        scores = {}
-        for t, h in [(1, 0), (2, 0), (3, 0), (0, 0), (1, 1), (2, 1), (3, 1), (0, 1)]:
-            scores[t, h] = psum.tile([P, JW], F32, name="s_ps", tag="bank%d" % (2 * t + h))
+        halves = [psum.tile([P, JW], F32, name="s1_ps%d" % h, tag="bank%d" % h) for h in range(2)]
+        whole = {t: psum.tile([P, S], F32, name="s_ps%d" % t, tag="bank%d" % bank) for bank, t in ((2, 0), (3, 2), (4, 3))}
+        for t, h in [(1, 0), (0, 0), (1, 1), (0, 1), (2, 0), (2, 1), (3, 0), (3, 1)]:
             nc.tensor.matmul_mx(
-                out=scores[t, h][:],
+                out=halves[h][:] if t == 1 else whole[t][:, h * JW : (h + 1) * JW],
                 lhsT=d_codes[:, t * P : (t + 1) * P].bitcast(FP8X4),
                 lhsT_scale=d_plane[:, t * P : (t + 1) * P],
                 rhs=x_codes[h][:].bitcast(FP8X4),
@@ -111,6 +116,7 @@ def tile_picked_scorebias_sigmoid_p_kernel(
                 start=True,
                 stop=True,
             )
+        scores = {(1, 0): halves[0], (1, JW): halves[1], (0, 0): whole[0], (2, 0): whole[2], (3, 0): whole[3]}
 
         w_codes = keep.tile([P, N], U32, name="w_codes", tag="stationary", align_bytes=64)
         w_plane = keep.tile([P, N], U8, name="w_plane", align_bytes=64)
@@ -128,58 +134,48 @@ def tile_picked_scorebias_sigmoid_p_kernel(
             )
 
         logit = keep.tile([P, PACK, S], F32, name="logit")
-        scaled = [None] + [keep.tile([P, S], F32, name="scaled%d" % t) for t in range(1, PACK)]
+        scaled = {t: keep.tile([P, S], F32, name="scaled%d" % t) for t in range(1, PACK)}
 
-        def leave(t, h):
-            nc.scalar.activation(scaled[t][:, h * JW : (h + 1) * JW], scores[t, h][:], ACT.Copy, scale=0.0625)
+        def leave(t, a, b):
+            nc.scalar.activation(scaled[t][:, a:b], scores[t, a][:], ACT.Copy, scale=0.0625)
 
         def add_bias(t, a, b):
             nc.vector.tensor_tensor(logit[:, t, a:b], tab_t[t][:].indirect(rel_t[:, a // 16 : b // 16]), scaled[t][:, a:b], ALU.add)
 
         bias0 = keep.tile([P, S], F32, name="bias0")
-        nc.vector.tensor_copy(bias0[:], tab_t[0][:].indirect(rel_t[:]))
-        load_tab(3, nc.sync)
-        for t in range(1, PACK):
-            for h in range(2):
-                leave(t, h)
-        cast_w(0)
-        cast_w(1)
-        add_bias(1, 0, S)
-        for h in range(2):
-            cols = slice(h * JW, (h + 1) * JW)
-            nc.vector.scalar_tensor_tensor(logit[:, 0, cols], scores[0, h][:], 0.0625, bias0[:, cols], ALU.mult, ALU.add)
-        add_bias(2, 0, S)
-        quant_w(0)
-        add_bias(3, 0, JW)
-        add_bias(3, JW, S)
-        quant_w(1)
 
         QW = S // 4
-        chunks = [(q * QW, (q + 1) * QW) for q in range(4)]
         sig = [keep.tile([P, QW, PACK], F32, name="sig%d" % q) for q in range(4)]
-        z_bf = keep.tile([P, S, PACK], BF16, name="z_bf", align_bytes=64)
+        z_bf = [keep.tile([P, JW, PACK], BF16, name="z_bf%d" % h, align_bytes=64) for h in range(2)]
+        chunks = [(q * QW, (q + 1) * QW) for q in range(4)]
         z_codes = [keep.tile([P, b - a], U32, name="z_codes%d" % a, align_bytes=64) for a, b in chunks]
         z_plane = [keep.tile([P, b - a], U8, name="z_plane%d" % a, align_bytes=64) for a, b in chunks]
 
-        def weigh(q):
+        def squash(q):
             nc.scalar.activation(
                 sig[q][:].rearrange("p (c i) t -> p c t i", i=4),
                 logit[:, :, q * QW : (q + 1) * QW].rearrange("p t (c i) -> p c t i", i=4),
                 ACT.Sigmoid,
             )
-            nc.vector.tensor_tensor(z_bf[:, q * QW : (q + 1) * QW, :], sig[q][:], gn_t[:].to_broadcast([P, QW, PACK]), ALU.mult)
+
+        def weigh(q):
+            nc.vector.tensor_tensor(
+                z_bf[q // 2][:, (q % 2) * QW : (q % 2 + 1) * QW, :], sig[q][:], gn_t[:].to_broadcast([P, QW, PACK]), ALU.mult
+            )
 
         def quant_z(c):
             a, b = chunks[c]
             nc.vector.quantize_mx(
-                out=z_codes[c][:].bitcast(FP8X4), scales=z_plane[c][:], in_=z_bf[:, a:b, :].rearrange("p j t -> p (j t)")
+                out=z_codes[c][:].bitcast(FP8X4),
+                scales=z_plane[c][:],
+                in_=z_bf[a // JW][:, a % JW : a % JW + b - a, :].rearrange("p j t -> p (j t)"),
             )
 
         out_view = out.rearrange("(m p) j -> p m j", p=P)
 
         def product(c, pair, engine, queue):
             a, b = chunks[c]
-            bank = psum.tile([P, 2, b - a], F32, name="o_ps", tag="bank%d" % ((2 * c + pair + 2) % 8))
+            bank = psum.tile([P, 2, b - a], F32, name="o_ps", tag="bank%d" % ((2 * c + pair + 5) % 8))
             for e in range(2):
                 m = 2 * pair + e
                 nc.tensor.matmul_mx(
@@ -195,15 +191,44 @@ def tile_picked_scorebias_sigmoid_p_kernel(
             engine(res[:], bank[:])
             queue.dma_start(out_view[:, 2 * pair : 2 * pair + 2, a:b], res[:])
 
+        nc.vector.tensor_copy(bias0[:], tab_t[0][:].indirect(rel_t[:]))
+        leave(1, 0, JW)
+        leave(1, JW, S)
+        leave(2, 0, S)
+        leave(3, 0, S)
+        cast_w(0)
+        cast_w(1)
+        add_bias(1, 0, S)
+        nc.vector.scalar_tensor_tensor(logit[:, 0, :], scores[0, 0][:], 0.0625, bias0[:], ALU.mult, ALU.add)
+        add_bias(2, 0, S)
+        quant_w(0)
+        add_bias(3, 0, JW)
+        squash(0)
+        squash(1)
+        add_bias(3, JW, S)
+        squash(2)
+        squash(3)
+        quant_w(1)
+        idle = psum.tile([P, N], F32, name="idle_ps", tag="bank3")
+        for e in range(2):
+            nc.tensor.matmul_mx(
+                out=idle[:],
+                lhsT=x_codes[e][:, 0:P].bitcast(FP8X4),
+                lhsT_scale=x_plane[:, e * JW : e * JW + P],
+                rhs=w_codes[:].bitcast(FP8X4),
+                rhs_scale=w_plane[:],
+                start=True,
+                stop=True,
+            )
         weigh(0)
         weigh(1)
         quant_z(0)
         weigh(2)
         quant_z(1)
-        quant_z(2)
-        weigh(3)
         product(0, 0, nc.scalar.copy, nc.sync)
-        product(0, 1, nc.vector.tensor_copy, nc.sync)
+        product(0, 1, nc.scalar.copy, nc.sync)
+        weigh(3)
+        quant_z(2)
         quant_z(3)
         product(1, 0, nc.scalar.copy, nc.sync)
         product(1, 1, nc.scalar.copy, nc.sync)

@@ -209,17 +209,6 @@ def tile_picked_scorebias_sigmoid_p_kernel(
         squash(2)
         squash(3)
         quant_w(1)
-        idle = psum.tile([P, N], F32, name="idle_ps", tag="bank3")
-        for e in range(2):
-            nc.tensor.matmul_mx(
-                out=idle[:],
-                lhsT=x_codes[e][:, 0:P].bitcast(FP8X4),
-                lhsT_scale=x_plane[:, e * JW : e * JW + P],
-                rhs=w_codes[:].bitcast(FP8X4),
-                rhs_scale=w_plane[:],
-                start=True,
-                stop=True,
-            )
         weigh(0)
         weigh(1)
         quant_z(0)

@@ -78,10 +78,10 @@ def tile_picked_scorebias_sigmoid_p_kernel(
         )
         nc.vector.tensor_copy(planes[:, H : H + S].bitcast(I32), xs_got[:].bitcast(I32))
         for a in range(1, 4):
-            nc.scalar.dma_start(planes[a:P:32, :].bitcast(I32), planes[8 * a : P : 32, :].bitcast(I32))
-        load_tab(1, nc.scalar)
+            nc.sync.dma_start(planes[a:P:32, :].bitcast(I32), planes[8 * a : P : 32, :].bitcast(I32))
+        load_tab(1, nc.sync)
         w_raw = [placed.tile([P, PACK, MW], F32, name="w_raw0", offset=4 * U, align_bytes=64)]
-        nc.scalar.dma_start(w_raw[0][:], w_view[:, :, 0:MW])
+        nc.sync.dma_start(w_raw[0][:], w_view[:, :, 0:MW])
         d_plane = planes[:, 0:H]
         x_plane = planes[:, H : H + S]
 

@@ -53,10 +53,10 @@ def tile_picked_scorebias_sigmoid_p_kernel(
         nc.sync.dma_start(kidx_t[:], kidx)
         nc.sync.dma_start(offs_t[:], offs)
         d_src = d_words[0].rearrange("p n t -> p (n t)").bitcast(I32)
-        nc.sync.dma_start(dw_win[:, 0 : G // 4], d_src[:, 0 : G // 4])
+        nc.sync.dma_start(dw_win[:, 0 : G // 8], d_src[:, 0 : G // 8])
         nc.sync.dma_start(ds_win[0:P:8, :].bitcast(I32), d_scales[0].bitcast(I32))
         nc.sync.dma_start(xs_win[0:P:8, :].bitcast(I32), x_scales[0].bitcast(I32))
-        nc.sync.dma_start(dw_win[:, G // 4 : G], d_src[:, G // 4 : G])
+        nc.sync.dma_start(dw_win[:, G // 8 : G], d_src[:, G // 8 : G])
         nc.sync.dma_start(xw_win[:], x_words[0].rearrange("p n t -> p (n t)").bitcast(I32))
 
         tab_t = []

@@ -209,6 +209,17 @@ def tile_picked_scorebias_sigmoid_p_kernel(
         squash(2)
         squash(3)
         quant_w(1)
+        for rep in range(2):
+            unread = psum.tile([P, N], F32, name="unread", tag="bank4")
+            nc.tensor.matmul_mx(
+                out=unread[:],
+                lhsT=x_codes[0][:, 0:P].bitcast(FP8X4),
+                lhsT_scale=x_plane[:, 0:P],
+                rhs=w_codes[:].bitcast(FP8X4),
+                rhs_scale=w_plane[:],
+                start=True,
+                stop=True,
+            )
         weigh(0)
         weigh(1)
         quant_z(0)

@@ -41,8 +41,7 @@ def tile_picked_scorebias_sigmoid_p_kernel(
         dw_win = placed.tile([P, G], I32, name="dw_win", offset=8 * U, align_bytes=64)
         xw_win = keep.tile([P, T], I32, name="xw_win", tag="slot_w1", align_bytes=64)
         for win in (ds_win, xs_win):
-            nc.gpsimd.memset(win[:, 0 : T // 2].bitcast(I32), 0)
-            nc.vector.memset(win[:, T // 2 : T].bitcast(I32), 0)
+            nc.vector.memset(win[:].bitcast(I32), 0)
         warm = keep.tile([P, 2], F32, name="warm")
         nc.vector.memset(warm[:, 0:1], 0.0)
         nc.scalar.activation(warm[:, 1:2], warm[:, 0:1], ACT.Sigmoid)

@@ -18,8 +18,10 @@ ALU = mybir.AluOpType
 P = 128
 PACK = 4
 JW = S // 2
+QW = S // 4
 MW = N // 2
-TAB_AT = [16 * U, 0, 8 * U, 20 * U]
+KIB = 1024
+WARM_PASSES = 3
 
 
 def tile_picked_scorebias_sigmoid_p_kernel(
@@ -38,8 +40,8 @@ def tile_picked_scorebias_sigmoid_p_kernel(
 
         ds_win = keep.tile([P, G], U8, name="ds_win", align_bytes=64)
         xs_win = keep.tile([P, T], U8, name="xs_win", align_bytes=64)
-        dw_win = placed.tile([P, G], I32, name="dw_win", offset=8 * U, align_bytes=64)
-        xw_win = keep.tile([P, T], I32, name="xw_win", tag="slot_w1", align_bytes=64)
+        dw_win = placed.tile([P, G], I32, name="dw_win", offset=12 * KIB + 64, align_bytes=64)
+        xw_win = keep.tile([P, T], I32, name="xw_win", align_bytes=64)
         for win in (ds_win, xs_win):
             nc.vector.memset(win[:].bitcast(I32), 0)
         warm = keep.tile([P, 2], F32, name="warm")
@@ -51,24 +53,25 @@ def tile_picked_scorebias_sigmoid_p_kernel(
 
         nc.sync.dma_start(kidx_t[:], kidx)
         nc.sync.dma_start(offs_t[:], offs)
+        nc.sync.dma_start(rel_t[:], rel)
         d_src = d_words[0].rearrange("p n t -> p (n t)").bitcast(I32)
         nc.sync.dma_start(dw_win[:, 0 : G // 8], d_src[:, 0 : G // 8])
         nc.sync.dma_start(ds_win[0:P:8, :].bitcast(I32), d_scales[0].bitcast(I32))
         nc.sync.dma_start(xs_win[0:P:8, :].bitcast(I32), x_scales[0].bitcast(I32))
         nc.sync.dma_start(dw_win[:, G // 8 : G], d_src[:, G // 8 : G])
-        nc.sync.dma_start(xw_win[:], x_words[0].rearrange("p n t -> p (n t)").bitcast(I32))
 
+        tab_at = [22 * KIB, 0, 4 * KIB + 64, 8 * KIB + 128]
         tab_t = []
 
-        def load_tab(t, queue):
-            tab_t.append(placed.tile([P, U], F32, name="tab%d" % t, offset=TAB_AT[t], align_bytes=64))
-            queue.dma_start(tab_t[t][:], tab_view[t])
+        def load_tab(t):
+            tab_t.append(placed.tile([P, U], F32, name="tab%d" % t, offset=tab_at[t], align_bytes=64))
+            nc.sync.dma_start(tab_t[t][:], tab_view[t])
 
-        load_tab(0, nc.sync)
-        nc.sync.dma_start(rel_t[:], rel)
+        nc.sync.dma_start(xw_win[:], x_words[0].rearrange("p n t -> p (n t)").bitcast(I32))
+        load_tab(0)
 
         ds_got = keep.tile([P, H], U8, name="ds_got", align_bytes=64)
-        xs_got = placed.tile([P, S], U8, name="xs_got", offset=4 * U - S // 2, align_bytes=64)
+        xs_got = placed.tile([P, S], U8, name="xs_got", offset=4 * KIB - 256, align_bytes=64)
         planes = keep.tile([P, H + S], U8, name="planes", align_bytes=64)
         nc.vector.tensor_copy(ds_got[:], ds_win[:].indirect(kidx_t[:]))
         nc.vector.tensor_copy(xs_got[:], xs_win[:].indirect(offs_t[:]))
@@ -78,53 +81,60 @@ def tile_picked_scorebias_sigmoid_p_kernel(
         nc.vector.tensor_copy(planes[:, H : H + S].bitcast(I32), xs_got[:].bitcast(I32))
         for a in range(1, 4):
             nc.sync.dma_start(planes[a:P:32, :].bitcast(I32), planes[8 * a : P : 32, :].bitcast(I32))
-        load_tab(1, nc.sync)
-        w_raw = [placed.tile([P, PACK, MW], F32, name="w_raw0", offset=4 * U, align_bytes=64)]
-        nc.sync.dma_start(w_raw[0][:], w_view[:, :, 0:MW])
+        load_tab(1)
+        load_tab(2)
         d_plane = planes[:, 0:H]
         x_plane = planes[:, H : H + S]
 
-        dw_got = placed.tile([P, H], U32, name="dw_got", offset=23 * U, align_bytes=64)
-        d_codes = keep.tile([P, H], U32, name="d_codes", tag="stationary", align_bytes=64)
+        dw_got = placed.tile([P, H], U32, name="dw_got", offset=33 * KIB, align_bytes=64)
+        d_codes = keep.tile([P, H], U32, name="d_codes", align_bytes=64)
         nc.vector.tensor_copy(dw_got[:], dw_win[:].bitcast(U32).indirect(kidx_t[:]))
-        load_tab(2, nc.sync)
-        w_raw.append(placed.tile([P, PACK, MW], F32, name="w_raw1", offset=12 * U, align_bytes=64))
-        nc.sync.dma_start(w_raw[1][:], w_view[:, :, MW:N])
+        load_tab(3)
         nc.vector.tensor_copy(
             d_codes[:].rearrange("p (t c i) -> p c t i", t=PACK, i=4), dw_got[:].rearrange("p (c i t) -> p c t i", t=PACK, i=4)
         )
-        load_tab(3, nc.sync)
-        gn_t = placed.tile([P, 1, PACK], F32, name="gn_t", offset=24 * U, align_bytes=64)
+        w_raw = [placed.tile([P, PACK, MW], F32, name="w_raw0", offset=30 * KIB, align_bytes=64)]
+        nc.sync.dma_start(w_raw[0][:], w_view[:, :, 0:MW])
+        gn_t = placed.tile([P, 1, PACK], F32, name="gn_t", offset=34 * KIB, align_bytes=64)
         nc.sync.dma_start(gn_t[:, 0, :], gn.rearrange("(p t) o -> p (t o)", t=PACK))
+        w_raw.append(placed.tile([P, PACK, MW], F32, name="w_raw1", offset=34 * KIB + 64, align_bytes=64))
+        nc.sync.dma_start(w_raw[1][:], w_view[:, :, MW:N])
 
-        x_codes = [keep.tile([P, JW], U32, name="x_codes%d" % h, align_bytes=64) for h in range(2)]
-        for h in range(2):
-            nc.vector.tensor_copy(
-                x_codes[h][:], xw_win[:].bitcast(U32).indirect(offs_t[:, h * JW // 16 : (h + 1) * JW // 16])
-            )
+        x_codes = keep.tile([P, S], U32, name="x_codes", align_bytes=64)
+        for a in (0, JW):
+            nc.vector.tensor_copy(x_codes[:, a : a + JW], xw_win[:].bitcast(U32).indirect(offs_t[:, a // 16 : (a + JW) // 16]))
 
-        halves = [psum.tile([P, JW], F32, name="s1_ps%d" % h, tag="bank%d" % h) for h in range(2)]
-        whole = {t: psum.tile([P, S], F32, name="s_ps%d" % t, tag="bank%d" % bank) for bank, t in ((2, 0), (3, 2), (4, 3))}
-        for t, h in [(1, 0), (0, 0), (1, 1), (0, 1), (2, 0), (2, 1), (3, 0), (3, 1)]:
+        scores = {}
+
+        def score(bank, t, a, b):
+            scores[t, a] = psum.tile([P, b - a], F32, name="s_ps%d%d" % (t, a), tag="bank%d" % bank)
             nc.tensor.matmul_mx(
-                out=halves[h][:] if t == 1 else whole[t][:, h * JW : (h + 1) * JW],
+                out=scores[t, a][:],
                 lhsT=d_codes[:, t * P : (t + 1) * P].bitcast(FP8X4),
                 lhsT_scale=d_plane[:, t * P : (t + 1) * P],
-                rhs=x_codes[h][:].bitcast(FP8X4),
-                rhs_scale=x_plane[:, h * JW : (h + 1) * JW],
+                rhs=x_codes[:, a:b].bitcast(FP8X4),
+                rhs_scale=x_plane[:, a:b],
                 start=True,
                 stop=True,
             )
-        scores = {(1, 0): halves[0], (1, JW): halves[1], (0, 0): whole[0], (2, 0): whole[2], (3, 0): whole[3]}
 
-        w_codes = keep.tile([P, N], U32, name="w_codes", tag="stationary", align_bytes=64)
+        for bank, (t, a, b) in enumerate([(1, 0, JW), (3, 0, JW), (0, 0, S), (1, JW, S), (2, 0, JW), (3, JW, S)]):
+            score(bank, t, a, b)
+
+        def scores_at(t, a, b):
+            return scores[t, a][:, 0 : b - a] if (t, a) in scores else scores[t, 0][:, a:b]
+
+        w_codes = keep.tile([P, N], U32, name="w_codes", align_bytes=64)
         w_plane = keep.tile([P, N], U8, name="w_plane", align_bytes=64)
-        w_bf = [keep.tile([P, MW * PACK], BF16, name="w_bf%d" % c, align_bytes=64) for c in range(2)]
+        w_bf = [
+            placed.tile([P, MW * PACK], BF16, name="w_bf%d" % c, offset=at, align_bytes=64)
+            for c, at in enumerate((50 * KIB, 48 * KIB))
+        ]
 
-        def cast_w(c):
-            nc.scalar.copy(
-                w_bf[c][:].rearrange("p (c i t) -> p c t i", i=4, t=PACK),
-                w_raw[c][:].rearrange("p t (c i) -> p c t i", i=4),
+        def cast_w(c, a, b, engine):
+            engine(
+                w_bf[c][:, a * PACK : b * PACK].rearrange("p (c i t) -> p c t i", i=4, t=PACK),
+                w_raw[c][:, :, a:b].rearrange("p t (c i) -> p c t i", i=4),
             )
 
         def quant_w(c):
@@ -132,106 +142,124 @@ def tile_picked_scorebias_sigmoid_p_kernel(
                 out=w_codes[:, c * MW : (c + 1) * MW].bitcast(FP8X4), scales=w_plane[:, c * MW : (c + 1) * MW], in_=w_bf[c][:]
             )
 
-        logit = keep.tile([P, PACK, S], F32, name="logit")
-        scaled = {t: keep.tile([P, S], F32, name="scaled%d" % t) for t in range(1, PACK)}
+        logit = keep.tile([P, 2, PACK, JW], F32, name="logit")
+        bias_at = {(0, 0): 25, (0, 1): 26, (1, 0): 27, (1, 1): 28, (2, 1): 29, (2, 0): 31, (3, 1): 32}
+        bias = {}
 
-        def leave(t, a, b):
-            nc.scalar.activation(scaled[t][:, a:b], scores[t, a][:], ACT.Copy, scale=0.0625)
+        def bias_tile(t, a, b):
+            bias[t, a] = placed.tile([P, b - a], F32, name="bias%d%d" % (t, a), offset=(bias_at[t, a // JW] + 15) * KIB, align_bytes=64)
+            return bias[t, a]
 
-        def add_bias(t, a, b):
-            nc.vector.tensor_tensor(logit[:, t, a:b], tab_t[t][:].indirect(rel_t[:, a // 16 : b // 16]), scaled[t][:, a:b], ALU.add)
 
-        bias0 = keep.tile([P, S], F32, name="bias0")
+        def fetch_s(t, a, b):
+            nc.scalar.activation(bias_tile(t, a, b)[:], tab_t[t][:].indirect(rel_t[:, a // 16 : b // 16]), ACT.Copy)
 
-        QW = S // 4
+        def add(t, a, b):
+            looked_up = bias[t, a][:, 0 : b - a] if (t, a) in bias else bias[t, 0][:, a:b]
+            nc.vector.scalar_tensor_tensor(
+                logit[:, a // JW : b // JW, t, :],
+                scores_at(t, a, b).rearrange("p (h j) -> p h j", j=JW),
+                0.0625,
+                looked_up.rearrange("p (h j) -> p h j", j=JW),
+                ALU.mult,
+                ALU.add,
+            )
+
+        scaled = {t: keep.tile([P, JW], F32, name="scaled%d" % t) for t in (1, 3)}
+
+        def leave(t):
+            nc.vector.tensor_scalar(scaled[t][:], scores_at(t, 0, JW), 0.0625, None, ALU.mult)
+
+        def fetch_add(t):
+            nc.vector.tensor_tensor(logit[:, 0, t, :], tab_t[t][:].indirect(rel_t[:, 0 : JW // 16]), scaled[t][:], ALU.add)
+
         sig = [keep.tile([P, QW, PACK], F32, name="sig%d" % q) for q in range(4)]
-        z_bf = [keep.tile([P, JW, PACK], BF16, name="z_bf%d" % h, align_bytes=64) for h in range(2)]
-        chunks = [(q * QW, (q + 1) * QW) for q in range(4)]
-        z_codes = [keep.tile([P, b - a], U32, name="z_codes%d" % a, align_bytes=64) for a, b in chunks]
-        z_plane = [keep.tile([P, b - a], U8, name="z_plane%d" % a, align_bytes=64) for a, b in chunks]
+        z_bf = [keep.tile([P, QW, PACK], BF16, name="z_bf%d" % q, align_bytes=64) for q in range(4)]
+        z_codes = [keep.tile([P, QW], U32, name="z_codes%d" % q, align_bytes=64) for q in range(4)]
+        z_plane = [keep.tile([P, QW], U8, name="z_plane%d" % q, align_bytes=64) for q in range(4)]
 
         def squash(q):
             nc.scalar.activation(
                 sig[q][:].rearrange("p (c i) t -> p c t i", i=4),
-                logit[:, :, q * QW : (q + 1) * QW].rearrange("p t (c i) -> p c t i", i=4),
+                logit[:, q // 2, :, q % 2 * QW : (q % 2 + 1) * QW].rearrange("p t (c i) -> p c t i", i=4),
                 ACT.Sigmoid,
             )
 
         def weigh(q):
-            nc.vector.tensor_tensor(
-                z_bf[q // 2][:, (q % 2) * QW : (q % 2 + 1) * QW, :], sig[q][:], gn_t[:].to_broadcast([P, QW, PACK]), ALU.mult
-            )
+            nc.vector.tensor_tensor(z_bf[q][:], sig[q][:], gn_t[:].to_broadcast([P, QW, PACK]), ALU.mult)
 
-        def quant_z(c):
-            a, b = chunks[c]
+        def quant_z(q):
             nc.vector.quantize_mx(
-                out=z_codes[c][:].bitcast(FP8X4),
-                scales=z_plane[c][:],
-                in_=z_bf[a // JW][:, a % JW : a % JW + b - a, :].rearrange("p j t -> p (j t)"),
+                out=z_codes[q][:].bitcast(FP8X4), scales=z_plane[q][:], in_=z_bf[q][:].rearrange("p j t -> p (j t)")
             )
 
         out_view = out.rearrange("(m p) j -> p m j", p=P)
 
-        def product(c, pair, engine, queue):
-            a, b = chunks[c]
-            bank = psum.tile([P, 2, b - a], F32, name="o_ps", tag="bank%d" % ((2 * c + pair + 5) % 8))
+        def product(q, pair, engine, queue):
+            bank = psum.tile([P, 2, QW], F32, name="o_ps", tag="bank%d" % ((2 * q + pair + 6) % 8))
             for e in range(2):
                 m = 2 * pair + e
                 nc.tensor.matmul_mx(
                     out=bank[:, e, :],
                     lhsT=w_codes[:, m * P : (m + 1) * P].bitcast(FP8X4),
                     lhsT_scale=w_plane[:, m * P : (m + 1) * P],
-                    rhs=z_codes[c][:].bitcast(FP8X4),
-                    rhs_scale=z_plane[c][:],
+                    rhs=z_codes[q][:].bitcast(FP8X4),
+                    rhs_scale=z_plane[q][:],
                     start=True,
                     stop=True,
                 )
-            res = keep.tile([P, 2, b - a], F32, name="res%d%d" % (c, pair))
+            res = keep.tile([P, 2, QW], F32, name="res%d%d" % (q, pair))
             engine(res[:], bank[:])
-            queue.dma_start(out_view[:, 2 * pair : 2 * pair + 2, a:b], res[:])
+            queue.dma_start(out_view[:, 2 * pair : 2 * pair + 2, q * QW : (q + 1) * QW], res[:])
 
-        nc.vector.tensor_copy(bias0[:], tab_t[0][:].indirect(rel_t[:]))
-        leave(1, 0, JW)
-        leave(1, JW, S)
-        leave(2, 0, S)
-        leave(3, 0, S)
-        cast_w(0)
-        cast_w(1)
-        add_bias(1, 0, S)
-        nc.vector.scalar_tensor_tensor(logit[:, 0, :], scores[0, 0][:], 0.0625, bias0[:], ALU.mult, ALU.add)
-        add_bias(2, 0, S)
-        quant_w(0)
-        add_bias(3, 0, JW)
+        fetch_s(0, 0, S)
+        leave(1)
+        leave(3)
+        add(0, 0, S)
+        fetch_s(1, JW, S)
+        fetch_add(1)
+        add(1, JW, S)
+        fetch_s(2, 0, JW)
+        fetch_s(2, JW, S)
+        add(2, 0, JW)
+        score(4, 2, JW, S)
+        fetch_s(3, JW, S)
+        fetch_add(3)
         squash(0)
         squash(1)
-        add_bias(3, JW, S)
+        add(2, JW, S)
+        add(3, JW, S)
+        cast_w(0, 0, MW, nc.vector.tensor_copy)
         squash(2)
         squash(3)
-        quant_w(1)
-        for rep in range(2):
-            unread = psum.tile([P, N], F32, name="unread", tag="bank4")
+        cast_w(1, P, MW, nc.scalar.copy)
+        weigh(0)
+        quant_w(0)
+        quant_z(0)
+        weigh(1)
+        cast_w(1, 0, P, nc.vector.tensor_copy)
+        quant_z(1)
+        product(0, 0, nc.scalar.copy, nc.sync)
+        unread = psum.tile([P, WARM_PASSES, QW], F32, name="unread", tag="bank5")
+        for rep in range(WARM_PASSES):
             nc.tensor.matmul_mx(
-                out=unread[:],
-                lhsT=x_codes[0][:, 0:P].bitcast(FP8X4),
-                lhsT_scale=x_plane[:, 0:P],
-                rhs=w_codes[:].bitcast(FP8X4),
-                rhs_scale=w_plane[:],
+                out=unread[:, rep, :],
+                lhsT=w_codes[:, 0:P].bitcast(FP8X4),
+                lhsT_scale=w_plane[:, 0:P],
+                rhs=z_codes[0][:].bitcast(FP8X4),
+                rhs_scale=z_plane[0][:],
                 start=True,
                 stop=True,
             )
-        weigh(0)
-        weigh(1)
-        quant_z(0)
+        product(1, 0, nc.scalar.copy, nc.sync)
         weigh(2)
-        quant_z(1)
-        product(0, 0, nc.scalar.copy, nc.sync)
+        quant_w(1)
+        quant_z(2)
         product(0, 1, nc.scalar.copy, nc.sync)
         weigh(3)
-        quant_z(2)
+        product(1, 1, nc.vector.tensor_copy, nc.sync)
         quant_z(3)
-        product(1, 0, nc.scalar.copy, nc.sync)
-        product(1, 1, nc.scalar.copy, nc.sync)
         product(2, 0, nc.scalar.copy, nc.sync)
-        product(2, 1, nc.vector.tensor_copy, nc.sync)
+        product(2, 1, nc.scalar.copy, nc.sync)
         product(3, 0, nc.vector.tensor_copy, nc.sync)
         product(3, 1, nc.scalar.copy, nc.scalar)

@@ -52,12 +52,12 @@ def tile_picked_scorebias_sigmoid_p_kernel(
         tab_view = tab.rearrange("(p t) u -> t p u", t=PACK)
 
         nc.sync.dma_start(kidx_t[:], kidx)
-        nc.sync.dma_start(offs_t[:], offs)
-        nc.sync.dma_start(rel_t[:], rel)
         d_src = d_words[0].rearrange("p n t -> p (n t)").bitcast(I32)
         nc.sync.dma_start(dw_win[:, 0 : G // 8], d_src[:, 0 : G // 8])
         nc.sync.dma_start(ds_win[0:P:8, :].bitcast(I32), d_scales[0].bitcast(I32))
+        nc.sync.dma_start(offs_t[:], offs)
         nc.sync.dma_start(xs_win[0:P:8, :].bitcast(I32), x_scales[0].bitcast(I32))
+        nc.sync.dma_start(rel_t[:], rel)
         nc.sync.dma_start(dw_win[:, G // 8 : G], d_src[:, G // 8 : G])
 
         tab_at = [22 * KIB, 0, 4 * KIB + 64, 8 * KIB + 128]

@@ -57,7 +57,6 @@ def tile_picked_scorebias_sigmoid_p_kernel(
         nc.sync.dma_start(ds_win[0:P:8, :].bitcast(I32), d_scales[0].bitcast(I32))
         nc.sync.dma_start(offs_t[:], offs)
         nc.sync.dma_start(xs_win[0:P:8, :].bitcast(I32), x_scales[0].bitcast(I32))
-        nc.sync.dma_start(rel_t[:], rel)
         nc.sync.dma_start(dw_win[:, G // 8 : G], d_src[:, G // 8 : G])
 
         tab_at = [22 * KIB, 0, 4 * KIB + 64, 8 * KIB + 128]
@@ -68,6 +67,7 @@ def tile_picked_scorebias_sigmoid_p_kernel(
             nc.sync.dma_start(tab_t[t][:], tab_view[t])
 
         nc.sync.dma_start(xw_win[:], x_words[0].rearrange("p n t -> p (n t)").bitcast(I32))
+        nc.sync.dma_start(rel_t[:], rel)
         load_tab(0)
 
         ds_got = keep.tile([P, H], U8, name="ds_got", align_bytes=64)
@@ -91,7 +91,7 @@ def tile_picked_scorebias_sigmoid_p_kernel(
         nc.vector.tensor_copy(dw_got[:], dw_win[:].bitcast(U32).indirect(kidx_t[:]))
         load_tab(3)
         nc.vector.tensor_copy(
-            d_codes[:].rearrange("p (t c i) -> p c t i", t=PACK, i=4), dw_got[:].rearrange("p (c i t) -> p c t i", t=PACK, i=4)
+            d_codes[:].rearrange("p (t c i) -> p c t i", t=PACK, i=2), dw_got[:].rearrange("p (c i t) -> p c t i", t=PACK, i=2)
         )
         w_raw = [placed.tile([P, PACK, MW], F32, name="w_raw0", offset=30 * KIB, align_bytes=64)]
         nc.sync.dma_start(w_raw[0][:], w_view[:, :, 0:MW])
@@ -133,8 +133,8 @@ def tile_picked_scorebias_sigmoid_p_kernel(
 
         def cast_w(c, a, b, engine):
             engine(
-                w_bf[c][:, a * PACK : b * PACK].rearrange("p (c i t) -> p c t i", i=4, t=PACK),
-                w_raw[c][:, :, a:b].rearrange("p t (c i) -> p c t i", i=4),
+                w_bf[c][:, a * PACK : b * PACK].rearrange("p (c i t) -> p c t i", i=2, t=PACK),
+                w_raw[c][:, :, a:b].rearrange("p t (c i) -> p c t i", i=2),
             )
 
         def quant_w(c):
@@ -180,8 +180,8 @@ def tile_picked_scorebias_sigmoid_p_kernel(
 
         def squash(q):
             nc.scalar.activation(
-                sig[q][:].rearrange("p (c i) t -> p c t i", i=4),
-                logit[:, q // 2, :, q % 2 * QW : (q % 2 + 1) * QW].rearrange("p t (c i) -> p c t i", i=4),
+                sig[q][:].rearrange("p (c i) t -> p c t i", i=2),
+                logit[:, q // 2, :, q % 2 * QW : (q % 2 + 1) * QW].rearrange("p t (c i) -> p c t i", i=2),
                 ACT.Sigmoid,
             )
 

@@ -17,11 +17,28 @@ ALU = mybir.AluOpType
 
 P = 128
 PACK = 4
+LIST_ROWS = 16
+SCORE_SCALE = 0.0625
 JW = S // 2
 QW = S // 4
 MW = N // 2
-KIB = 1024
+NEAR = 2
+D_FIRST = G // 8
 WARM_PASSES = 3
+KIB = 1024
+
+XS_GOT_AT = 4 * KIB - 256
+DW_WIN_AT = 12 * KIB + 64
+TAB_AT = (22 * KIB, 0, 4 * KIB + 64, 8 * KIB + 128)
+DW_GOT_AT = 33 * KIB
+W_RAW_AT = (30 * KIB, 34 * KIB + 64)
+GN_AT = 34 * KIB
+BIAS_AT = {(0, 0): 40 * KIB, (1, JW): 43 * KIB, (2, JW): 44 * KIB, (2, 0): 46 * KIB, (3, JW): 47 * KIB}
+W_BF_AT = (50 * KIB, 48 * KIB)
+
+BANKS = 8
+FIRST_OUT_BANK = 6
+WARM_BANK = 5
 
 
 def tile_picked_scorebias_sigmoid_p_kernel(
@@ -34,13 +51,16 @@ def tile_picked_scorebias_sigmoid_p_kernel(
         placed = ctx.enter_context(tc.tile_pool(name="placed", bufs=1))
         psum = ctx.enter_context(tc.psum_pool(name="psum", bufs=1))
 
-        kidx_t = lists.tile([P, H // 16], U16, name="kidx_t")
-        offs_t = lists.tile([P, S // 16], U16, name="offs_t")
-        rel_t = lists.tile([P, S // 16], U16, name="rel_t")
+        kidx_t = lists.tile([P, H // LIST_ROWS], U16, name="kidx_t")
+        offs_t = lists.tile([P, S // LIST_ROWS], U16, name="offs_t")
+        rel_t = lists.tile([P, S // LIST_ROWS], U16, name="rel_t")
+
+        def entries(list_tile, a, b):
+            return list_tile[:, a // LIST_ROWS : b // LIST_ROWS]
 
         ds_win = keep.tile([P, G], U8, name="ds_win", align_bytes=64)
         xs_win = keep.tile([P, T], U8, name="xs_win", align_bytes=64)
-        dw_win = placed.tile([P, G], I32, name="dw_win", offset=12 * KIB + 64, align_bytes=64)
+        dw_win = placed.tile([P, G], I32, name="dw_win", offset=DW_WIN_AT, align_bytes=64)
         xw_win = keep.tile([P, T], I32, name="xw_win", align_bytes=64)
         for win in (ds_win, xs_win):
             nc.vector.memset(win[:].bitcast(I32), 0)
@@ -52,18 +72,17 @@ def tile_picked_scorebias_sigmoid_p_kernel(
         tab_view = tab.rearrange("(p t) u -> t p u", t=PACK)
 
         nc.sync.dma_start(kidx_t[:], kidx)
-        d_src = d_words[0].rearrange("p n t -> p (n t)").bitcast(I32)
-        nc.sync.dma_start(dw_win[:, 0 : G // 8], d_src[:, 0 : G // 8])
-        nc.sync.dma_start(ds_win[0:P:8, :].bitcast(I32), d_scales[0].bitcast(I32))
         nc.sync.dma_start(offs_t[:], offs)
+        d_src = d_words[0].rearrange("p n t -> p (n t)").bitcast(I32)
+        nc.sync.dma_start(ds_win[0:P:8, :].bitcast(I32), d_scales[0].bitcast(I32))
+        nc.sync.dma_start(dw_win[:, 0:D_FIRST], d_src[:, 0:D_FIRST])
         nc.sync.dma_start(xs_win[0:P:8, :].bitcast(I32), x_scales[0].bitcast(I32))
-        nc.sync.dma_start(dw_win[:, G // 8 : G], d_src[:, G // 8 : G])
+        nc.sync.dma_start(dw_win[:, D_FIRST:G], d_src[:, D_FIRST:G])
 
-        tab_at = [22 * KIB, 0, 4 * KIB + 64, 8 * KIB + 128]
         tab_t = []
 
         def load_tab(t):
-            tab_t.append(placed.tile([P, U], F32, name="tab%d" % t, offset=tab_at[t], align_bytes=64))
+            tab_t.append(placed.tile([P, U], F32, name="tab%d" % t, offset=TAB_AT[t], align_bytes=64))
             nc.sync.dma_start(tab_t[t][:], tab_view[t])
 
         nc.sync.dma_start(xw_win[:], x_words[0].rearrange("p n t -> p (n t)").bitcast(I32))
@@ -71,7 +90,7 @@ def tile_picked_scorebias_sigmoid_p_kernel(
         load_tab(0)
 
         ds_got = keep.tile([P, H], U8, name="ds_got", align_bytes=64)
-        xs_got = placed.tile([P, S], U8, name="xs_got", offset=4 * KIB - 256, align_bytes=64)
+        xs_got = placed.tile([P, S], U8, name="xs_got", offset=XS_GOT_AT, align_bytes=64)
         planes = keep.tile([P, H + S], U8, name="planes", align_bytes=64)
         nc.vector.tensor_copy(ds_got[:], ds_win[:].indirect(kidx_t[:]))
         nc.vector.tensor_copy(xs_got[:], xs_win[:].indirect(offs_t[:]))
@@ -86,23 +105,24 @@ def tile_picked_scorebias_sigmoid_p_kernel(
         d_plane = planes[:, 0:H]
         x_plane = planes[:, H : H + S]
 
-        dw_got = placed.tile([P, H], U32, name="dw_got", offset=33 * KIB, align_bytes=64)
+        dw_got = placed.tile([P, H], U32, name="dw_got", offset=DW_GOT_AT, align_bytes=64)
         d_codes = keep.tile([P, H], U32, name="d_codes", align_bytes=64)
         nc.vector.tensor_copy(dw_got[:], dw_win[:].bitcast(U32).indirect(kidx_t[:]))
         load_tab(3)
         nc.vector.tensor_copy(
-            d_codes[:].rearrange("p (t c i) -> p c t i", t=PACK, i=2), dw_got[:].rearrange("p (c i t) -> p c t i", t=PACK, i=2)
+            d_codes[:].rearrange("p (t c i) -> p c t i", t=PACK, i=NEAR),
+            dw_got[:].rearrange("p (c i t) -> p c t i", t=PACK, i=NEAR),
         )
-        w_raw = [placed.tile([P, PACK, MW], F32, name="w_raw0", offset=30 * KIB, align_bytes=64)]
+        w_raw = [placed.tile([P, PACK, MW], F32, name="w_raw0", offset=W_RAW_AT[0], align_bytes=64)]
         nc.sync.dma_start(w_raw[0][:], w_view[:, :, 0:MW])
-        gn_t = placed.tile([P, 1, PACK], F32, name="gn_t", offset=34 * KIB, align_bytes=64)
+        gn_t = placed.tile([P, 1, PACK], F32, name="gn_t", offset=GN_AT, align_bytes=64)
         nc.sync.dma_start(gn_t[:, 0, :], gn.rearrange("(p t) o -> p (t o)", t=PACK))
-        w_raw.append(placed.tile([P, PACK, MW], F32, name="w_raw1", offset=34 * KIB + 64, align_bytes=64))
+        w_raw.append(placed.tile([P, PACK, MW], F32, name="w_raw1", offset=W_RAW_AT[1], align_bytes=64))
         nc.sync.dma_start(w_raw[1][:], w_view[:, :, MW:N])
 
         x_codes = keep.tile([P, S], U32, name="x_codes", align_bytes=64)
         for a in (0, JW):
-            nc.vector.tensor_copy(x_codes[:, a : a + JW], xw_win[:].bitcast(U32).indirect(offs_t[:, a // 16 : (a + JW) // 16]))
+            nc.vector.tensor_copy(x_codes[:, a : a + JW], xw_win[:].bitcast(U32).indirect(entries(offs_t, a, a + JW)))
 
         scores = {}
 
@@ -118,23 +138,20 @@ def tile_picked_scorebias_sigmoid_p_kernel(
                 stop=True,
             )
 
-        for bank, (t, a, b) in enumerate([(1, 0, JW), (3, 0, JW), (0, 0, S), (1, JW, S), (2, 0, JW), (3, JW, S)]):
+        early_scores = [(1, 0, JW), (3, 0, JW), (0, 0, S), (1, JW, S), (2, 0, JW), (3, JW, S)]
+        for bank, (t, a, b) in enumerate(early_scores):
             score(bank, t, a, b)
-
-        def scores_at(t, a, b):
-            return scores[t, a][:, 0 : b - a] if (t, a) in scores else scores[t, 0][:, a:b]
 
         w_codes = keep.tile([P, N], U32, name="w_codes", align_bytes=64)
         w_plane = keep.tile([P, N], U8, name="w_plane", align_bytes=64)
         w_bf = [
-            placed.tile([P, MW * PACK], BF16, name="w_bf%d" % c, offset=at, align_bytes=64)
-            for c, at in enumerate((50 * KIB, 48 * KIB))
+            placed.tile([P, MW * PACK], BF16, name="w_bf%d" % c, offset=at, align_bytes=64) for c, at in enumerate(W_BF_AT)
         ]
 
-        def cast_w(c, a, b, engine):
-            engine(
-                w_bf[c][:, a * PACK : b * PACK].rearrange("p (c i t) -> p c t i", i=2, t=PACK),
-                w_raw[c][:, :, a:b].rearrange("p t (c i) -> p c t i", i=2),
+        def cast_w(c, a, b, copy):
+            copy(
+                w_bf[c][:, a * PACK : b * PACK].rearrange("p (c i t) -> p c t i", i=NEAR, t=PACK),
+                w_raw[c][:, :, a:b].rearrange("p t (c i) -> p c t i", i=NEAR),
             )
 
         def quant_w(c):
@@ -143,35 +160,29 @@ def tile_picked_scorebias_sigmoid_p_kernel(
             )
 
         logit = keep.tile([P, 2, PACK, JW], F32, name="logit")
-        bias_at = {(0, 0): 25, (0, 1): 26, (1, 0): 27, (1, 1): 28, (2, 1): 29, (2, 0): 31, (3, 1): 32}
         bias = {}
 
-        def bias_tile(t, a, b):
-            bias[t, a] = placed.tile([P, b - a], F32, name="bias%d%d" % (t, a), offset=(bias_at[t, a // JW] + 15) * KIB, align_bytes=64)
-            return bias[t, a]
-
-
-        def fetch_s(t, a, b):
-            nc.scalar.activation(bias_tile(t, a, b)[:], tab_t[t][:].indirect(rel_t[:, a // 16 : b // 16]), ACT.Copy)
+        def fetch(t, a, b):
+            bias[t, a] = placed.tile([P, b - a], F32, name="bias%d%d" % (t, a), offset=BIAS_AT[t, a], align_bytes=64)
+            nc.scalar.activation(bias[t, a][:], tab_t[t][:].indirect(entries(rel_t, a, b)), ACT.Copy)
 
         def add(t, a, b):
-            looked_up = bias[t, a][:, 0 : b - a] if (t, a) in bias else bias[t, 0][:, a:b]
             nc.vector.scalar_tensor_tensor(
                 logit[:, a // JW : b // JW, t, :],
-                scores_at(t, a, b).rearrange("p (h j) -> p h j", j=JW),
-                0.0625,
-                looked_up.rearrange("p (h j) -> p h j", j=JW),
+                scores[t, a][:].rearrange("p (h j) -> p h j", j=JW),
+                SCORE_SCALE,
+                bias[t, a][:].rearrange("p (h j) -> p h j", j=JW),
                 ALU.mult,
                 ALU.add,
             )
 
         scaled = {t: keep.tile([P, JW], F32, name="scaled%d" % t) for t in (1, 3)}
 
-        def leave(t):
-            nc.vector.tensor_scalar(scaled[t][:], scores_at(t, 0, JW), 0.0625, None, ALU.mult)
+        def scale_out(t):
+            nc.vector.tensor_scalar(scaled[t][:], scores[t, 0][:], SCORE_SCALE, None, ALU.mult)
 
         def fetch_add(t):
-            nc.vector.tensor_tensor(logit[:, 0, t, :], tab_t[t][:].indirect(rel_t[:, 0 : JW // 16]), scaled[t][:], ALU.add)
+            nc.vector.tensor_tensor(logit[:, 0, t, :], tab_t[t][:].indirect(entries(rel_t, 0, JW)), scaled[t][:], ALU.add)
 
         sig = [keep.tile([P, QW, PACK], F32, name="sig%d" % q) for q in range(4)]
         z_bf = [keep.tile([P, QW, PACK], BF16, name="z_bf%d" % q, align_bytes=64) for q in range(4)]
@@ -180,8 +191,8 @@ def tile_picked_scorebias_sigmoid_p_kernel(
 
         def squash(q):
             nc.scalar.activation(
-                sig[q][:].rearrange("p (c i) t -> p c t i", i=2),
-                logit[:, q // 2, :, q % 2 * QW : (q % 2 + 1) * QW].rearrange("p t (c i) -> p c t i", i=2),
+                sig[q][:].rearrange("p (c i) t -> p c t i", i=NEAR),
+                logit[:, q // 2, :, q % 2 * QW : (q % 2 + 1) * QW].rearrange("p t (c i) -> p c t i", i=NEAR),
                 ACT.Sigmoid,
             )
 
@@ -195,40 +206,43 @@ def tile_picked_scorebias_sigmoid_p_kernel(
 
         out_view = out.rearrange("(m p) j -> p m j", p=P)
 
-        def product(q, pair, engine, queue):
-            bank = psum.tile([P, 2, QW], F32, name="o_ps", tag="bank%d" % ((2 * q + pair + 6) % 8))
-            for e in range(2):
-                m = 2 * pair + e
-                nc.tensor.matmul_mx(
-                    out=bank[:, e, :],
-                    lhsT=w_codes[:, m * P : (m + 1) * P].bitcast(FP8X4),
-                    lhsT_scale=w_plane[:, m * P : (m + 1) * P],
-                    rhs=z_codes[q][:].bitcast(FP8X4),
-                    rhs_scale=z_plane[q][:],
-                    start=True,
-                    stop=True,
-                )
-            res = keep.tile([P, 2, QW], F32, name="res%d%d" % (q, pair))
-            engine(res[:], bank[:])
-            queue.dma_start(out_view[:, 2 * pair : 2 * pair + 2, q * QW : (q + 1) * QW], res[:])
+        def multiply(dst, m, q):
+            nc.tensor.matmul_mx(
+                out=dst,
+                lhsT=w_codes[:, m * P : (m + 1) * P].bitcast(FP8X4),
+                lhsT_scale=w_plane[:, m * P : (m + 1) * P],
+                rhs=z_codes[q][:].bitcast(FP8X4),
+                rhs_scale=z_plane[q][:],
+                start=True,
+                stop=True,
+            )
 
-        fetch_s(0, 0, S)
-        leave(1)
-        leave(3)
+        def product(q, c, copy, queue):
+            bank = psum.tile([P, 2, QW], F32, name="o_ps", tag="bank%d" % ((2 * q + c + FIRST_OUT_BANK) % BANKS))
+            for e in range(2):
+                multiply(bank[:, e, :], 2 * c + e, q)
+            res = keep.tile([P, 2, QW], F32, name="res%d%d" % (q, c))
+            copy(res[:], bank[:])
+            queue.dma_start(out_view[:, 2 * c : 2 * c + 2, q * QW : (q + 1) * QW], res[:])
+
+        fetch(0, 0, S)
+        scale_out(1)
+        scale_out(3)
         add(0, 0, S)
-        fetch_s(1, JW, S)
+        fetch(1, JW, S)
         fetch_add(1)
         add(1, JW, S)
-        fetch_s(2, 0, JW)
-        fetch_s(2, JW, S)
+        fetch(2, 0, JW)
+        fetch(2, JW, S)
         add(2, 0, JW)
-        score(4, 2, JW, S)
-        fetch_s(3, JW, S)
+        score(early_scores.index((2, 0, JW)), 2, JW, S)
+        fetch(3, JW, S)
         fetch_add(3)
         squash(0)
         squash(1)
         add(2, JW, S)
         add(3, JW, S)
+
         cast_w(0, 0, MW, nc.vector.tensor_copy)
         squash(2)
         squash(3)
@@ -240,17 +254,9 @@ def tile_picked_scorebias_sigmoid_p_kernel(
         cast_w(1, 0, P, nc.vector.tensor_copy)
         quant_z(1)
         product(0, 0, nc.scalar.copy, nc.sync)
-        unread = psum.tile([P, WARM_PASSES, QW], F32, name="unread", tag="bank5")
+        unread = psum.tile([P, WARM_PASSES, QW], F32, name="unread", tag="bank%d" % WARM_BANK)
         for rep in range(WARM_PASSES):
-            nc.tensor.matmul_mx(
-                out=unread[:, rep, :],
-                lhsT=w_codes[:, 0:P].bitcast(FP8X4),
-                lhsT_scale=w_plane[:, 0:P],
-                rhs=z_codes[0][:].bitcast(FP8X4),
-                rhs_scale=z_plane[0][:],
-                start=True,
-                stop=True,
-            )
+            multiply(unread[:, rep, :], 0, 0)
         product(1, 0, nc.scalar.copy, nc.sync)
         weigh(2)
         quant_w(1)

from contextlib import ExitStack

import concourse.mybir as mybir

K, T, S, N, G, H, U = 512, 2048, 512, 512, 2048, 512, 1024
FLOPS = 2 * K * H * S + 2 * H * N * S

F32 = mybir.dt.float32
BF16 = mybir.dt.bfloat16
I32 = mybir.dt.int32
U32 = mybir.dt.uint32
U16 = mybir.dt.uint16
U8 = mybir.dt.uint8
FP8X4 = mybir.dt.float8_e4m3fn_x4
ACT = mybir.ActivationFunctionType
ALU = mybir.AluOpType

P = 128
PACK = 4
LIST_ROWS = 16
SCORE_SCALE = 0.0625
JW = S // 2
QW = S // 4
MW = N // 2
NEAR = 2
D_FIRST = G // 8
WARM_PASSES = 3
KIB = 1024

XS_GOT_AT = 4 * KIB - 256
DW_WIN_AT = 12 * KIB + 64
TAB_AT = (22 * KIB, 0, 4 * KIB + 64, 8 * KIB + 128)
DW_GOT_AT = 33 * KIB
W_RAW_AT = (30 * KIB, 34 * KIB + 64)
GN_AT = 34 * KIB
BIAS_AT = {(0, 0): 40 * KIB, (1, JW): 43 * KIB, (2, JW): 44 * KIB, (2, 0): 46 * KIB, (3, JW): 47 * KIB}
W_BF_AT = (50 * KIB, 48 * KIB)

BANKS = 8
FIRST_OUT_BANK = 6
WARM_BANK = 5


def tile_picked_scorebias_sigmoid_p_kernel(
    tc, x_words, x_scales, d_words, d_scales, tab, gn, w1, offs, kidx, rel, out
):
    nc = tc.nc
    with ExitStack() as ctx:
        lists = ctx.enter_context(tc.tile_pool(name="lists", bufs=1))
        keep = ctx.enter_context(tc.tile_pool(name="keep", bufs=1))
        placed = ctx.enter_context(tc.tile_pool(name="placed", bufs=1))
        psum = ctx.enter_context(tc.psum_pool(name="psum", bufs=1))

        kidx_t = lists.tile([P, H // LIST_ROWS], U16, name="kidx_t")
        offs_t = lists.tile([P, S // LIST_ROWS], U16, name="offs_t")
        rel_t = lists.tile([P, S // LIST_ROWS], U16, name="rel_t")

        def entries(list_tile, a, b):
            return list_tile[:, a // LIST_ROWS : b // LIST_ROWS]

        ds_win = keep.tile([P, G], U8, name="ds_win", align_bytes=64)
        xs_win = keep.tile([P, T], U8, name="xs_win", align_bytes=64)
        dw_win = placed.tile([P, G], I32, name="dw_win", offset=DW_WIN_AT, align_bytes=64)
        xw_win = keep.tile([P, T], I32, name="xw_win", align_bytes=64)
        for win in (ds_win, xs_win):
            nc.vector.memset(win[:].bitcast(I32), 0)
        warm = keep.tile([P, 2], F32, name="warm")
        nc.vector.memset(warm[:, 0:1], 0.0)
        nc.scalar.activation(warm[:, 1:2], warm[:, 0:1], ACT.Sigmoid)

        w_view = w1.rearrange("(p t) m -> p t m", t=PACK)
        tab_view = tab.rearrange("(p t) u -> t p u", t=PACK)

        nc.sync.dma_start(kidx_t[:], kidx)
        nc.sync.dma_start(offs_t[:], offs)
        d_src = d_words[0].rearrange("p n t -> p (n t)").bitcast(I32)
        nc.sync.dma_start(ds_win[0:P:8, :].bitcast(I32), d_scales[0].bitcast(I32))
        nc.sync.dma_start(dw_win[:, 0:D_FIRST], d_src[:, 0:D_FIRST])
        nc.sync.dma_start(xs_win[0:P:8, :].bitcast(I32), x_scales[0].bitcast(I32))
        nc.sync.dma_start(dw_win[:, D_FIRST:G], d_src[:, D_FIRST:G])

        tab_t = []

        def load_tab(t):
            tab_t.append(placed.tile([P, U], F32, name="tab%d" % t, offset=TAB_AT[t], align_bytes=64))
            nc.sync.dma_start(tab_t[t][:], tab_view[t])

        nc.sync.dma_start(xw_win[:], x_words[0].rearrange("p n t -> p (n t)").bitcast(I32))
        nc.sync.dma_start(rel_t[:], rel)
        load_tab(0)

        ds_got = keep.tile([P, H], U8, name="ds_got", align_bytes=64)
        xs_got = placed.tile([P, S], U8, name="xs_got", offset=XS_GOT_AT, align_bytes=64)
        planes = keep.tile([P, H + S], U8, name="planes", align_bytes=64)
        nc.vector.tensor_copy(ds_got[:], ds_win[:].indirect(kidx_t[:]))
        nc.vector.tensor_copy(xs_got[:], xs_win[:].indirect(offs_t[:]))
        nc.vector.tensor_copy(
            planes[:, 0:H].rearrange("p (t m) -> p t m", t=PACK), ds_got[:].rearrange("p (m t) -> p t m", t=PACK)
        )
        nc.vector.tensor_copy(planes[:, H : H + S].bitcast(I32), xs_got[:].bitcast(I32))
        for a in range(1, 4):
            nc.sync.dma_start(planes[a:P:32, :].bitcast(I32), planes[8 * a : P : 32, :].bitcast(I32))
        load_tab(1)
        load_tab(2)
        d_plane = planes[:, 0:H]
        x_plane = planes[:, H : H + S]

        dw_got = placed.tile([P, H], U32, name="dw_got", offset=DW_GOT_AT, align_bytes=64)
        d_codes = keep.tile([P, H], U32, name="d_codes", align_bytes=64)
        nc.vector.tensor_copy(dw_got[:], dw_win[:].bitcast(U32).indirect(kidx_t[:]))
        load_tab(3)
        nc.vector.tensor_copy(
            d_codes[:].rearrange("p (t c i) -> p c t i", t=PACK, i=NEAR),
            dw_got[:].rearrange("p (c i t) -> p c t i", t=PACK, i=NEAR),
        )
        w_raw = [placed.tile([P, PACK, MW], F32, name="w_raw0", offset=W_RAW_AT[0], align_bytes=64)]
        nc.sync.dma_start(w_raw[0][:], w_view[:, :, 0:MW])
        gn_t = placed.tile([P, 1, PACK], F32, name="gn_t", offset=GN_AT, align_bytes=64)
        nc.sync.dma_start(gn_t[:, 0, :], gn.rearrange("(p t) o -> p (t o)", t=PACK))
        w_raw.append(placed.tile([P, PACK, MW], F32, name="w_raw1", offset=W_RAW_AT[1], align_bytes=64))
        nc.sync.dma_start(w_raw[1][:], w_view[:, :, MW:N])

        x_codes = keep.tile([P, S], U32, name="x_codes", align_bytes=64)
        for a in (0, JW):
            nc.vector.tensor_copy(x_codes[:, a : a + JW], xw_win[:].bitcast(U32).indirect(entries(offs_t, a, a + JW)))

        scores = {}

        def score(bank, t, a, b):
            scores[t, a] = psum.tile([P, b - a], F32, name="s_ps%d%d" % (t, a), tag="bank%d" % bank)
            nc.tensor.matmul_mx(
                out=scores[t, a][:],
                lhsT=d_codes[:, t * P : (t + 1) * P].bitcast(FP8X4),
                lhsT_scale=d_plane[:, t * P : (t + 1) * P],
                rhs=x_codes[:, a:b].bitcast(FP8X4),
                rhs_scale=x_plane[:, a:b],
                start=True,
                stop=True,
            )

        early_scores = [(1, 0, JW), (3, 0, JW), (0, 0, S), (1, JW, S), (2, 0, JW), (3, JW, S)]
        for bank, (t, a, b) in enumerate(early_scores):
            score(bank, t, a, b)

        w_codes = keep.tile([P, N], U32, name="w_codes", align_bytes=64)
        w_plane = keep.tile([P, N], U8, name="w_plane", align_bytes=64)
        w_bf = [
            placed.tile([P, MW * PACK], BF16, name="w_bf%d" % c, offset=at, align_bytes=64) for c, at in enumerate(W_BF_AT)
        ]

        def cast_w(c, a, b, copy):
            copy(
                w_bf[c][:, a * PACK : b * PACK].rearrange("p (c i t) -> p c t i", i=NEAR, t=PACK),
                w_raw[c][:, :, a:b].rearrange("p t (c i) -> p c t i", i=NEAR),
            )

        def quant_w(c):
            nc.vector.quantize_mx(
                out=w_codes[:, c * MW : (c + 1) * MW].bitcast(FP8X4), scales=w_plane[:, c * MW : (c + 1) * MW], in_=w_bf[c][:]
            )

        logit = keep.tile([P, 2, PACK, JW], F32, name="logit")
        bias = {}

        def fetch(t, a, b):
            bias[t, a] = placed.tile([P, b - a], F32, name="bias%d%d" % (t, a), offset=BIAS_AT[t, a], align_bytes=64)
            nc.scalar.activation(bias[t, a][:], tab_t[t][:].indirect(entries(rel_t, a, b)), ACT.Copy)

        def add(t, a, b):
            nc.vector.scalar_tensor_tensor(
                logit[:, a // JW : b // JW, t, :],
                scores[t, a][:].rearrange("p (h j) -> p h j", j=JW),
                SCORE_SCALE,
                bias[t, a][:].rearrange("p (h j) -> p h j", j=JW),
                ALU.mult,
                ALU.add,
            )

        scaled = {t: keep.tile([P, JW], F32, name="scaled%d" % t) for t in (1, 3)}

        def scale_out(t):
            nc.vector.tensor_scalar(scaled[t][:], scores[t, 0][:], SCORE_SCALE, None, ALU.mult)

        def fetch_add(t):
            nc.vector.tensor_tensor(logit[:, 0, t, :], tab_t[t][:].indirect(entries(rel_t, 0, JW)), scaled[t][:], ALU.add)

        sig = [keep.tile([P, QW, PACK], F32, name="sig%d" % q) for q in range(4)]
        z_bf = [keep.tile([P, QW, PACK], BF16, name="z_bf%d" % q, align_bytes=64) for q in range(4)]
        z_codes = [keep.tile([P, QW], U32, name="z_codes%d" % q, align_bytes=64) for q in range(4)]
        z_plane = [keep.tile([P, QW], U8, name="z_plane%d" % q, align_bytes=64) for q in range(4)]

        def squash(q):
            nc.scalar.activation(
                sig[q][:].rearrange("p (c i) t -> p c t i", i=NEAR),
                logit[:, q // 2, :, q % 2 * QW : (q % 2 + 1) * QW].rearrange("p t (c i) -> p c t i", i=NEAR),
                ACT.Sigmoid,
            )

        def weigh(q):
            nc.vector.tensor_tensor(z_bf[q][:], sig[q][:], gn_t[:].to_broadcast([P, QW, PACK]), ALU.mult)

        def quant_z(q):
            nc.vector.quantize_mx(
                out=z_codes[q][:].bitcast(FP8X4), scales=z_plane[q][:], in_=z_bf[q][:].rearrange("p j t -> p (j t)")
            )

        out_view = out.rearrange("(m p) j -> p m j", p=P)

        def multiply(dst, m, q):
            nc.tensor.matmul_mx(
                out=dst,
                lhsT=w_codes[:, m * P : (m + 1) * P].bitcast(FP8X4),
                lhsT_scale=w_plane[:, m * P : (m + 1) * P],
                rhs=z_codes[q][:].bitcast(FP8X4),
                rhs_scale=z_plane[q][:],
                start=True,
                stop=True,
            )

        def product(q, c, copy, queue):
            bank = psum.tile([P, 2, QW], F32, name="o_ps", tag="bank%d" % ((2 * q + c + FIRST_OUT_BANK) % BANKS))
            for e in range(2):
                multiply(bank[:, e, :], 2 * c + e, q)
            res = keep.tile([P, 2, QW], F32, name="res%d%d" % (q, c))
            copy(res[:], bank[:])
            queue.dma_start(out_view[:, 2 * c : 2 * c + 2, q * QW : (q + 1) * QW], res[:])

        fetch(0, 0, S)
        scale_out(1)
        scale_out(3)
        add(0, 0, S)
        fetch(1, JW, S)
        fetch_add(1)
        add(1, JW, S)
        fetch(2, 0, JW)
        fetch(2, JW, S)
        add(2, 0, JW)
        score(early_scores.index((2, 0, JW)), 2, JW, S)
        fetch(3, JW, S)
        fetch_add(3)
        squash(0)
        squash(1)
        add(2, JW, S)
        add(3, JW, S)

        cast_w(0, 0, MW, nc.vector.tensor_copy)
        squash(2)
        squash(3)
        cast_w(1, P, MW, nc.scalar.copy)
        weigh(0)
        quant_w(0)
        quant_z(0)
        weigh(1)
        cast_w(1, 0, P, nc.vector.tensor_copy)
        quant_z(1)
        product(0, 0, nc.scalar.copy, nc.sync)
        unread = psum.tile([P, WARM_PASSES, QW], F32, name="unread", tag="bank%d" % WARM_BANK)
        for rep in range(WARM_PASSES):
            multiply(unread[:, rep, :], 0, 0)
        product(1, 0, nc.scalar.copy, nc.sync)
        weigh(2)
        quant_w(1)
        quant_z(2)
        product(0, 1, nc.scalar.copy, nc.sync)
        weigh(3)
        product(1, 1, nc.vector.tensor_copy, nc.sync)
        quant_z(3)
        product(2, 0, nc.scalar.copy, nc.sync)
        product(2, 1, nc.scalar.copy, nc.sync)
        product(3, 0, nc.vector.tensor_copy, nc.sync)
        product(3, 1, nc.scalar.copy, nc.scalar)
